import numpy as np, ml_dtypes
CORES = [5,29,101,125,133,157,229,253]
N = 8
BF = ml_dtypes.bfloat16
def gentries(a):
    return np.ascontiguousarray(a.reshape(8, 16, -1).transpose(0, 2, 1)).reshape(8, -1)
def gtable(e):
    e = np.asarray(e); return np.ascontiguousarray(e.reshape(8, -1, 16).transpose(0, 2, 1)).reshape(128, -1).astype(np.int32)
V, G, LN, RO, SH = 1280, 384, 64, 2, 4
DS = [1, 2, 6, 7]
W = V + len(DS) * G
def graph(rng, share):
    s = rng.permutation(4 * V); n = int(4 * V * share); n = n + n % 2
    b = np.empty(4 * V, np.int64); b[s[:n]] = rng.integers(V, W, n); p = s[n:].reshape(2, -1)
    b[p[0]] = p[1] % V; b[p[1]] = p[0] % V
    return b
def marks(rng, size=1.0):
    return ((0.25 + 0.75 * rng.random((N, 8, 16, V))) * size).astype(np.float32)
def parts(rng):
    x = rng.integers(0, 4096, (N, 8, 16, V))
    nb = np.stack([np.stack([graph(rng, float(rng.choice(np.array([0.05, 0.15, 0.25])))) for g in range(8)]) for q in range(N)])
    z = (N, 8, RO, LN); k = rng.integers(0, 4, z); j = np.where(rng.random(z) < 0.95, (k + rng.integers(1, 4, z)) % 4, k)
    la = np.stack([rng.integers(0, V, z), j, k, rng.integers(0, 4, z), rng.integers(1, 17, z)])
    return x, marks(rng), nb, la
def pack(x, am, nb, la):
    d = {"x": np.ascontiguousarray(x.reshape(N, 128, V)).astype(np.int32), "am": np.ascontiguousarray(am.reshape(N, 128, V)).astype(BF), "nb": np.stack([gtable(t) for t in nb])}
    for i, name in enumerate(("lb", "pj", "pk", "pl", "hq")): d[name] = np.stack([gtable(t.reshape(8, -1)) for t in la[i]])
    return d
def setup_inputs(rng):
    return pack(*parts(rng))
def setup_inputs_spread(rng):
    x, am, nb, la = parts(rng)
    u = np.minimum(np.exp2(12.0 * rng.random(x.shape)).astype(np.int64) - 1, 4095); side = rng.random((N, 8, 1, V)) < 0.5
    return pack(np.where(side, 4095 - u, u), marks(rng, np.exp2(rng.integers(-1, 2, (N, 8, 1, V)).astype(np.float64))), nb, la)
def setup_inputs_ends(rng):
    x, am, nb, la = parts(rng); flip = rng.random(16) < 0.5; flip[0] = False; flip[15] = True; M = V // 8; late = np.arange(4, M - 1, 4)
    for q in range(N):
        for g in range(8):
            o = np.arange(1, V - 1); o = rng.permutation(o[o != G - 1])
            t = o[:4 * M].reshape(4, M).copy(); t[1, 0] = 0; t[1, 1] = V - 1; A, B, C, D = t
            col = rng.integers(0, 2, V); col[G - 1] = 1; cb = rng.integers(0, 2, M); cb[0] = 0; cb[1] = 1
            col[B] = cb; col[D] = cb; col[A] = 1 - cb; col[C] = 1 - cb
            col[A[late]] = cb[late]; col[D[late]] = 1 - cb[late]
            n = np.repeat(np.where(col == 0, W - 1, 0)[None], 4, 0); r = rng.random((4, V)) < 0.05; r[:, t.reshape(-1)] = False
            n = np.where(r, rng.integers(0, W, (4, V)), n)
            k = 3 * rng.integers(0, 2, M); j = 3 - k
            n[k, B] = A; n[j, B] = C; n[k, C] = D; n[j, C] = B; n[j, A] = B; n[k, D] = C
            nb[q, g] = n.reshape(-1)
            v = np.repeat(col[None], 16, 0); odd = t[:, 3:M - 1:2].reshape(-1); v[:, odd] = rng.integers(0, 2, (16, len(odd)))
            x[q, g] = 4095 * np.where(flip[:, None], 1 - v, v)
            b = np.where(rng.random((RO, LN)) < 0.7, rng.integers(0, 2, (RO, LN)), rng.integers(2, M - 1, (RO, LN))); b[:, LN - 1] = M - 1; b[:, LN - 2] = M - 4
            void = rng.random((RO, LN)) < 0.1; void[:, LN - 2:] = False
            la[0, q, g] = B[b]; la[2, q, g] = k[b]; la[3, q, g] = k[b]; la[1, q, g] = np.where(void, k[b], j[b])
    la[4] = np.where(rng.random(la[4].shape) < 0.5, 1, 16)
    am = rng.choice(np.array([0.125, 4.0], np.float32), am.shape)
    return pack(x, am, nb, la)
def tie(rng, n, t, more):
    p = np.argsort(rng.random((4, t.shape[1], 4)), axis=-1); A, B, C, D = t
    for i, names in enumerate(([B] + more[0], [A, C] + more[1], [B, D] + more[2], [C] + more[3])):
        for s, name in enumerate(names): n[p[i, :, s], t[i]] = name
    return p[1, :, 1], p[1, :, 0], p[2, :, 1]
def setup_inputs_calm(rng):
    x, am, nb, la = parts(rng); K = RO * LN; ki = np.arange(K) % 16; nl = K // 16; nk = 11 * nl; Q = 2 ** SH; late = np.arange(nl) * 16 // LN
    am = (0.125 + 0.125 * rng.random(am.shape)).astype(np.float32)
    a1 = 4 * nk; a2 = a1 + 12 * nl; a3 = a2 + 16 * nl; a4 = a3 + 6; a5 = a4 + RO * (3 * RO + 1) // 2
    for q in range(N):
        for g in range(8):
            o = rng.permutation(V); n = nb[q, g].reshape(4, V); xs = x[q, g]
            rest = o[a5:]; few = rest[rest >= G][:64]; fa, fb, fc, fd = few.reshape(4, 16)
            n[np.isin(n, fb)] = o[a3]
            own = np.concatenate([o[:a5], few]); n[:, own] = own
            L = np.zeros((5, K), np.int64)
            t = o[:a1].reshape(4, nk); A, B, C, D = t; m = ki < 11
            L[1, m], L[2, m], L[3, m] = tie(rng, n, t, [[A] * 3, [B] * 2, [C] * 2, [D] * 3])
            v = rng.choice(np.array([0, 1, 2, 3, 8, 15, 16]), nk); up = np.argsort(rng.random((16, nk)), axis=0) < v
            base = rng.integers(0, 2048, (16, nk)); flat = rng.integers(0, 4096, (16, nk))
            for i, step in enumerate((0, 1024, 2048, 2048)): xs[:, t[i]] = np.where(up, base + step, flat)
            L[0, m] = B; L[4, m] = np.clip(v + rng.integers(0, 2, nk), 1, 16)
            c = o[a1:a2].reshape(2, 6, nl); m = ki == 15
            for h in range(2):
                for i in range(6):
                    n[0, c[h, i]] = c[h, max(i - 1, 0)]; n[3, c[h, i]] = c[h, min(i + 1, 5)]; xs[:, c[h, i]] = 819 * i
            n[1, c[0, 2]] = c[1, 2]; n[2, c[1, 2]] = c[0, 2]
            L[0, m] = c[0, 2]; L[1, m] = 1; L[4, m] = 1
            p = rng.integers(2, 2049, 16); far = rng.integers(p + 2047, 4096)
            va = int(rng.choice(np.array([1, 2, 3, 8, 15, 16]))); act = (np.argsort(rng.random(16)) < va).astype(np.int64)
            xs[:, o[a3:a4]] = np.stack([p, p - 1, p + 1, p - 2, far - 1, p + 1025], axis=1)
            h0, hm, hp, h2, hc, one = [int(u) for u in o[a3:a4]]
            z = a4; tip = np.zeros(RO, np.int64)
            for r in range(RO):
                s = o[z:z + 3 * r + 2]; z += 3 * r + 2
                for i in range(3 * r + 2): xs[:, s[i]] = p + 1024 * (1 - i % 2) + i * (Q - 1)
                xs[:, s[-1]] = xs[:, s[-1]] + act
                n[0, s[:-1]] = s[1:]; tip[r] = s[0]
            for e in range(4):
                t = o[a2 + 4 * nl * e:a2 + 4 * nl * (e + 1)].reshape(4, nl); A, B, C, D = t; m = ki == 11 + e
                if e in (0, 3):
                    for i, at in enumerate((p, p - 1, far, p)): xs[:, t[i]] = at[:, None]
                    more = [[hm, hp, hp], [h2, h0], [hc, hc], [hm, hp, hp]]
                    if e == 3: more[0] = [hp, tip[late], one]
                else:
                    for i in range(4): xs[:, t[i]] = p[:, None]
                    more = [[A] * 3, [B] * 2, [C] * 2, [D] * 3]; w = rng.integers(1, 4, nl)
                    if e == 1: more[0] = [one, np.where(w > 1, one, A), np.where(w > 2, one, A)]
                    if e == 2: more[0] = [tip[late], A, A]
                L[1, m], L[2, m], L[3, m] = tie(rng, n, t, more); L[0, m] = B
                L[4, m] = rng.integers(1, 17, nl) if e < 2 else np.minimum(va + np.arange(nl) % 2, 16)
            d = 1024 + np.where(rng.random((16, 16)) < 0.5, -1, 1) * rng.integers(900, 1017, (16, 16)); mid = rng.integers(d, 4096 - d); side = np.where(rng.random((16, 16)) < 0.5, -1, 1)
            xs[:, fa] = mid; xs[:, fb] = mid + side * d; xs[:, fc] = mid - side * d; xs[:, fd] = mid + side * d
            n[0, fa] = fb; n[1, fa] = fc; n[2, fa] = fb; n[3, fa] = fc; n[:, fb] = fd
            am[q, g][:, fb] = 4.0
            la[:, q, g] = L.reshape(5, RO, LN)
    return pack(x, am, nb, la)
def setup_inputs_corners(rng):
    x, am, nb, la = parts(rng)
    am = np.where(rng.random(am.shape) < 0.06, 0.125, np.exp2(-3.0 + 2.0 * rng.random(am.shape))).astype(np.float32)
    x = np.where(rng.random(x.shape) < 0.8, rng.choice(np.array([0, 1, 1023, 1024, 1025, 2047, 2048, 4094, 4095]), x.shape), x)
    for q in range(N):
        for g in range(8):
            n = nb[q, g].reshape(4, V); ty = (g + q) % 6
            if ty == 0: n[:] = rng.integers(V, W, (4, V))
            if ty == 1:
                for k in (0, 1, 3):
                    m = rng.permutation(V).reshape(2, -1); n[k, m[0]] = m[1]; n[k, m[1]] = m[0]
                n[2] = n[0]
            if ty == 2:
                m = rng.permutation(V)[:5 * (V // 10)].reshape(5, -1)
                for i in range(5):
                    for k in range(4): n[k, m[i]] = m[(i + 1 + k) % 5]
            if ty == 3: n[:] = rng.integers(0, V, (4, V))
            if ty == 4: n[:] = np.where(rng.random((4, V)) < 0.1, np.arange(V)[None], n)
            if ty == 5: n[:] = np.where(rng.random((4, V)) < 0.3, rng.choice(np.array([0, V - 1, V, W - 1]), (4, V)), n)
    la[0] = np.where(rng.random(la[0].shape) < 0.1, rng.choice(np.array([0, V - 1]), la[0].shape), la[0])
    la[4] = rng.choice(np.array([1, 2, 15, 16]), la[4].shape)
    return pack(x, am, nb, la)
def block(n, a, b, c, d):
    n[0, b] = a; n[3, b] = c; n[2, c] = b; n[0, c] = d; n[1, a] = b; n[2, d] = c
def setup_inputs_crowd(rng):
    x, am, nb, la = parts(rng)
    for q in range(N):
        for g in range(8):
            n = nb[q, g].reshape(4, V); ty = (g + q) % 5; o = rng.permutation(V); L = la[:, q, g]; z = int(rng.integers(0, 4))
            if ty <= 1:
                at = o[:2 * LN + 9]; n[:, at] = rng.integers(V, W, (4, len(at)))
                h = o[0]; D = o[1:5]; B = o[5:5 + LN]; A = o[5 + LN:5 + 2 * LN]
                n[:, h] = D; n[0, D] = h; n[0, B] = A; n[3, B] = h; n[1, A] = B
                for t in range(RO): L[0, t] = rng.permutation(B)
                L[1] = 3; L[2] = 0; L[1, 0, :z] = 0
                if ty == 1:
                    a, b, c, d = o[5 + 2 * LN:9 + 2 * LN]; block(n, a, b, c, d); L[0, :, LN - 1] = b; L[3, :, LN - 1] = 0
            if ty == 2:
                n[:, o[:4]] = rng.integers(V, W, (4, 4)); block(n, o[0], o[1], o[2], o[3])
                L[0] = o[1]; L[1] = 3; L[2] = 0; L[3] = 0; L[1, :, :z] = 0
            if ty == 3:
                m = o[:3 * LN + 1]; n[:, m] = rng.integers(V, W, (4, len(m))); n[0, m[1:]] = m[:-1]; n[3, m[:-1]] = m[1:]
                for t in range(RO): L[0, t] = m[3 * (np.arange(LN) if t == 0 else rng.permutation(LN)) + 1]
                L[1] = 3; L[2] = 0; L[3] = 3
            if ty == 4:
                e = int(rng.integers(1, RO)); L[1, e] = L[2, e]; L[4, e - 1, ::2] = 1
    return pack(x, am, nb, la)
def check_ranges(d):
    bad = []
    for k, lo, hi in (("x", 0, 4095), ("nb", 0, W - 1), ("lb", 0, V - 1), ("pj", 0, 3), ("pk", 0, 3), ("pl", 0, 3), ("hq", 1, 16)):
        if np.min(d[k]) < lo or np.max(d[k]) > hi: bad.append("range of " + k)
    m = np.asarray(d["am"]).astype(np.float32)
    if not np.all((m >= 0.125) & (m <= 4.0)): bad.append("range of am")
    return bad
def full(s, r):
    return np.concatenate([s[r]] + [np.roll(s[(r - DS[b]) % N], -b, axis=0)[..., :G] for b in range(len(DS))], axis=2)
def pick(w, n):
    return np.stack([w[g][:, n[g].reshape(-1)] for g in range(8)]).reshape(8, 16, 4, V)
def pulls(w, n):
    d = pick(w, n) - w[:, :, None, :V]
    return np.clip(d - 1024 * np.sign(d), -1023, 1023)
def sweep(s, n, stress):
    new, e = [], []
    for r in range(N):
        p = pulls(full(s, r), n[r])
        if stress: e.append(np.sum(p * p, axis=2))
        new.append(np.clip(s[r] + (np.sum(p, axis=2) >> SH), 0, 4095).astype(np.int32))
    return np.stack(new), e
def winners(n, B, j, k, l):
    A = n[k, B]; C = n[j, B]; c = np.minimum(C, V - 1); D = n[l, c]; a = np.minimum(A, V - 1); d = np.minimum(D, V - 1)
    pa = n[:, a] == B; pd = n[:, d] == C
    good = (A < V) & (C < V) & (D < V) & (A != B) & (A != C) & (A != D) & (B != C) & (B != D) & (C != D)
    good = good & np.any(pa, axis=0) & np.any(pd, axis=0) & ~np.any(n[:, a] == C, axis=0) & ~np.any(n[:, d] == B, axis=0)
    who = np.stack([A, B, C, D]); i = np.arange(LN); first = np.full(W, LN)
    np.minimum.at(first, who[:, good], np.broadcast_to(i, (4, LN))[:, good])
    w = np.nonzero(good & np.all(first[who] >= i, axis=0))[0]
    port = np.stack([np.argmax(pa, axis=0), k, l, np.argmax(pd, axis=0)])
    return w, who[:, w], (port * V + who)[:, w], np.stack([C, D, A, B])[:, w]
def reference(x, am, nb, lb, pj, pk, pl, hq):
    s = x.astype(np.int32).reshape(N, 8, 16, V)
    n = np.stack([gentries(t) for t in nb]).astype(np.int64).reshape(N, 8, 4, V)
    la = [np.stack([gentries(t) for t in u]).astype(np.int64).reshape(N, 8, RO, LN) for u in (lb, pj, pk, pl, hq)]
    for t in range(RO):
        s, e1 = sweep(s, n, True)
        done = []
        for r in range(N):
            for g in range(8):
                w, who, at, name = winners(n[r, g], la[0][r, g, t], la[1][r, g, t], la[2][r, g, t], la[3][r, g, t])
                flat = n[r, g].reshape(-1); old = flat[at]; flat[at] = name; done.append((r, g, w, who, at, old))
        s, e2 = sweep(s, n, False)
        s, e3 = sweep(s, n, True)
        for r, g, w, who, at, old in done:
            worse = np.sum(e3[r][g][:, who], axis=1) > np.sum(e1[r][g][:, who], axis=1)
            back = np.sum(worse, axis=0) >= la[4][r, g, t, w]
            flat = n[r, g].reshape(-1); flat[at[:, back]] = old[:, back]
    m = am.astype(np.float32).astype(np.float64).reshape(N, 8, 16, V); y = []
    for r in range(N):
        p = pulls(full(s, r), n[r]).astype(np.float64)
        y.append(np.sum(pick(full(m, r), n[r]) * np.exp(p * p * (-2.0 ** -19)), axis=2).reshape(128, V))
    return {"y": np.stack(y).astype(np.float32)}

def check_inputs(d):
    bad = list(check_ranges(d))
    if not bad:
        for name, y in reference(**d).items():
            for q in range(N):
                v = np.abs(np.asarray(y[q], np.float64)); s = np.sqrt(np.mean(v * v))
                if v.max() > 5 * s or s < 2.0 ** -2: bad.append('%s of rank %d is uneven or too small' % (name, q))
    return bad

@@ -1,0 +1,733 @@
+import math
+from concourse.bass import DstId, RemoteDMATransfer
+from concourse.mybir import AluOpType, AxisListType, ActivationFunctionType
+
+V, G, W = 1280, 384, 2816
+DS = [1, 2, 6, 7]
+H = G // 2
+M = 12582912.0
+C0 = 1408.0
+CH = [(0, 384), (384, 832), (832, 1280)]
+CM, NSET = 448, 3
+NP = 7
+F32, F16, B16, I32, U16 = "float32", "float16", "bfloat16", "int32", "uint16"
+
+
+def _sb(n, dt):
+    return ("sbuf", [128, n], dt)
+
+
+SCRATCH = {
+    "win": _sb(NP * W, F32), "mw": _sb(W, B16), "nbw": _sb(5376, F32), "xi": _sb(V, I32), "x16": _sb(2 * V, F16),
+    "nbi": _sb(320, I32), "nb16": _sb(320, F16), "off": _sb(5 * 320, U16), "off32": _sb(320, F32),
+    "d16": _sb(4 * NSET * CM, F16), "c16": _sb(4 * NSET * CM, F16), "s16": _sb(4 * NSET * CM, B16),
+    "m16": _sb(41 * 128, F16), "mb": _sb(16 * 128, B16), "i32m": _sb(128, F32), "ones": _sb(CM, B16),
+    "ji": _sb(128, I32), "jf": _sb(128, F32), "jt": _sb(256, F32), "pi": _sb(8, I32), "col": _sb(32, F32),
+    "mq": _sb(16, F32), "mr": _sb(4, F32), "tab": _sb(1296, I32),
+    "l32": _sb(40, I32), "lu": _sb(40, U16), "lf": _sb(40, F32), "rep": _sb(256, F32),
+    "lq16": _sb(8, F16), "w4": _sb(4, F32), "thr": _sb(64, F32), "spare": _sb(16, F32),
+    "ti": _sb(128, I32), "tb": _sb(128, F32), "tw": _sb(128, F32), "to": _sb(128, F32),
+    "o1": _sb(16, U16), "o1f": _sb(16, F32), "oc": _sb(4, U16), "o2": _sb(64, U16), "o3": _sb(16, U16), "o4": _sb(128, U16),
+    "osc": _sb(32, U16), "at16": _sb(512, F16), "nm16": _sb(1024, F16), "eb": _sb(256, B16), "eg": _sb(256, B16),
+    "gp16": _sb(192, F16), "eq": _sb(4096, B16), "sb": _sb(256, B16), "al": _sb(16, F32), "pt": _sb(32, F32),
+    "vt": _sb(16, F32), "dn": _sb(16, F32), "tm": _sb(128, F32), "thg": _sb(64, F32),
+    "wn16": _sb(128, F16), "hqw": _sb(128, F32), "wb": _sb(64, B16),
+    "xo": _sb(256, F16), "sq": _sb(1024, F32), "sf": _sb(64, F32),
+    "ld": _sb(1024, F16), "lc": _sb(1024, F16), "ls": _sb(1024, B16),
+    "hop": ("dram", [NP * 256, H], F32), "hopm": ("dram", [256, H], B16),
+}
+for _n in ("X0", "X1", "X2", "T0", "T1", "L0", "L1", "L2"):
+    SCRATCH[_n] = ("psum", [128, 512], F32)
+NDMA = 20
+SEMAPHORES = (["qv", "qa", "qt", "qg", "sent"] + ["arr%d" % s for s in range(NP + 1)] + ["rel%d" % s for s in range(NP + 1)]
+              + ["dma%d" % k for k in range(NDMA)])
+A = AluOpType
+AF = ActivationFunctionType
+CYC, PEC = 1.0e-3, 0.5e-3
+XLAT = 7.0
+HOP, LOOK, GAP, STEAL, IDLE = 0.15, 0.3, 2.0, 0.2, 0.15
+SUB = [(0, 384, 0), (384, 832, 1), (832, 1280, 2)]
+FSUB = [(0, 384, 0), (384, 832, 1), (832, 1152, 2), (1152, 1280, 2)]
+SIGNV, SIGNF = (), (1, 2)
+PASSES, LATER, LATEF = 2, 6.0, 3.0
+
+
+def R(name, lo=0, hi=None, st=1):
+    return (name, lo, SCRATCH[name][1][1] if hi is None else hi, st)
+
+
+def IND(w, o):
+    return ("*", w, o)
+
+
+def _n(r):
+    return 16 * _n(r[2]) if r[0] == "*" else (r[2] - r[1] + r[3] - 1) // r[3]
+
+
+def _ap(T, r):
+    if not isinstance(r, tuple):
+        return r
+    if r[0] == "*":
+        return _ap(T, r[1]).indirect(_ap(T, r[2]))
+    return T[r[0]][:, r[1]:r[2]] if r[3] == 1 else T[r[0]][:, r[1]:r[2]:r[3]]
+
+
+def _ps(r):
+    return r[0] != "*" and SCRATCH[r[0]][0] == "psum"
+
+
+def _two(r):
+    return r[0] != "*" and SCRATCH[r[0]][2] in (F16, B16, U16)
+
+
+def build():
+    ops = []
+    boost = [0.0]
+
+    def add(eng, fn, wr, rd, cost, ninc=1, after=(), sem=None):
+        w, r = [], []
+        for t in wr:
+            if t[0] == "*":
+                w.append(t[1]); r.append(t[2])
+            else:
+                w.append(t)
+        for t in rd:
+            if isinstance(t, tuple):
+                if t[0] == "*":
+                    r += [t[1], t[2]]
+                else:
+                    r.append(t)
+        ops.append({"eng": eng, "fn": fn, "w": w, "r": r, "cost": cost, "ninc": ninc, "after": list(after), "sem": sem, "boost": boost[0]})
+        return len(ops) - 1
+
+    def vcost(out, ins, base):
+        n = _n(out)
+        if out[0] == "*":
+            return 0.05 + 3.8 * n * CYC
+        if ins[0][0] == "*":
+            return 0.05 + 1.56 * n * CYC
+        return 0.02 + max(64, base * n) * CYC
+
+    def ts(out, a, s1, o0, s2=None, o1=None):
+        def fn(g, T):
+            if o1 is None:
+                return [g.vector.tensor_scalar(_ap(T, out), _ap(T, a), _ap(T, s1), None, o0)]
+            return [g.vector.tensor_scalar(_ap(T, out), _ap(T, a), _ap(T, s1), _ap(T, s2), o0, o1)]
+        return add("v", fn, [out], [a, s1, s2], vcost(out, [a], 0.5 if _two(out) and _two(a) else 1))
+
+    def tt(out, a, b, o):
+        return add("v", lambda g, T: [g.vector.tensor_tensor(_ap(T, out), _ap(T, a), _ap(T, b), o)], [out], [a, b],
+                   vcost(out, [a], 1 if _ps(a) or _ps(b) else 2))
+
+    def cp(out, a):
+        return add("v", lambda g, T: [g.vector.tensor_copy(_ap(T, out), _ap(T, a))], [out], [a],
+                   vcost(out, [a], 0.5 if _two(out) and _two(a) else 1))
+
+    def ms(out, c):
+        return add("v", lambda g, T: [g.vector.memset(_ap(T, out), c)], [out], [], vcost(out, [out], 1))
+
+    def red(out, a):
+        return add("v", lambda g, T: [g.vector.tensor_reduce(_ap(T, out), _ap(T, a), AxisListType.X, A.add)], [out], [a], 0.09)
+
+    def scan(out, a, b):
+        return add("v", lambda g, T: [g.vector.tensor_tensor_scan(_ap(T, out), _ap(T, a), _ap(T, b), 0.0, A.mult, A.add)],
+                   [out], [a, b], vcost(out, [a], 1))
+
+    def act(out, a, f, bias=None, scale=None, extra=0.0):
+        def fn(g, T):
+            kw = {}
+            if bias is not None:
+                kw["bias"] = _ap(T, bias)
+            if scale is not None:
+                kw["scale"] = _ap(T, scale)
+            return [g.scalar.activation(_ap(T, out), _ap(T, a), f, **kw)]
+        return add("a", fn, [out], [a, bias, scale], 0.065 + extra + max(64, _n(out) * (1.56 if a[0] == "*" else 1)) * CYC)
+
+    ts1, cp1, act1 = ts, cp, act
+
+    def both(i, j):
+        o = ops.pop(j)
+        ops[i]["alt"] = (o["eng"], o["fn"], o["cost"])
+        return i
+
+    def flt(*rs):
+        return all(SCRATCH[(r[1] if r[0] == "*" else r)[0]][2] in (F32, F16, B16) for r in rs) and rs[0][0] != "*"
+
+    def act(out, a, f, bias=None, scale=None, extra=0.0):
+        i = act1(out, a, f, bias, scale, extra)
+        if f == AF.Copy:
+            return both(i, cp1(out, a) if scale is None else ts1(out, a, scale, A.mult))
+        if f == AF.Identity:
+            return both(i, ts1(out, a, bias, A.add))
+        if f == AF.Sign:
+            return both(i, ts1(out, a, -1.0, A.max, 1.0, A.min))
+        return i
+
+    def cp(out, a):
+        i = cp1(out, a)
+        return both(i, act1(out, a, AF.Copy)) if flt(out, a) else i
+
+    def ts(out, a, s1, o0, s2=None, o1=None):
+        i = ts1(out, a, s1, o0, s2, o1)
+        if flt(out, a) and o1 is None and o0 == A.mult and not (isinstance(s1, tuple) and _ps(s1)):
+            return both(i, act1(out, a, AF.Copy, scale=s1))
+        if flt(out, a) and (s1, s2) == (-1.0, 1.0):
+            return both(i, act1(out, a, AF.Sign))
+        return i
+
+    def mm(items, first=True, last=True):
+        def fn(g, T):
+            res = []
+            for k, (o, l, r) in enumerate(items):
+                st = first if k == 0 else items[k - 1][0] != o
+                sp = last if k == len(items) - 1 else items[k + 1][0] != o
+                res.append(g.tensor.matmul(_ap(T, o), _ap(T, l), _ap(T, r), st, sp))
+            return res
+        cost = 0.03 + sum(max(64, _n(r)) * PEC * (4 if SCRATCH[r[0]][2] == F32 else 1) for _, _, r in items)
+        return add("t", fn, [o for o, _, _ in items], [l for _, l, _ in items] + [r for _, _, r in items], cost, len(items))
+
+    ndma = [0]
+
+    def dma(fn, wr, rd, cost=2.2):
+        ndma[0] += 1
+        return add("s", fn, wr, rd, cost, sem="dma%d" % (ndma[0] - 1))
+
+    def exchange(s, src, dst):
+        k = add("g", ("send", s), [], [src], 0.6, ninc=0)
+        add("x", ("arr", s), [dst], [], XLAT, after=[k], sem="arr%d" % s)
+        return k
+
+    def m16(k):
+        return R("m16", 128 * k, 128 * k + 128)
+
+    def mb(k):
+        return R("mb", 128 * k, 128 * k + 128)
+
+    def col(k):
+        return R("col", k, k + 1)
+
+    SEL, DIAG, NI16, CF, CW, I16, I16S = 0, 16, 32, 33, 37, 39, 40
+    N64, N1024, CMI, MI, LTRI, WAD, BM4, WPA, WPD, BLK, IB, LW, NMI = 0, 1, 2, 3, 4, 5, 6, 7, 8, 9, 10, 11, 15
+    cP, cG, cI, cR, cT, cQ4, cTQ, cFA, cFC, cFB, cFD, cAD = range(12)
+
+    def win(s, lo=0, hi=W):
+        return R("win", s * W + lo, s * W + hi)
+
+    def diag(out, name, lo, hi):
+        return [(out, m16(DIAG + i), R(name, lo + i, hi, 16)) for i in range(16)]
+
+    dma(lambda q, T: q.dma_start(T.xi[:, 0:G], T.x[:, 0:G]), [R("xi", 0, G)], [])
+    dma(lambda q, T: q.dma_start(T.nbi[:], T.nb[:]), [R("nbi")], [])
+    dma(lambda q, T: q.dma_start(T.xi[:, G:V], T.x[:, G:V]), [R("xi", G, V)], [], 2.8)
+    for k, nm in enumerate(("lb", "pk", "pl", "hq", "pj")):
+        dma(lambda q, T, k=k, nm=nm: q.dma_start(T.l32[:, 8 * k:8 * k + 8], T[nm][:]), [R("l32", 8 * k, 8 * k + 8)], [])
+    dma(lambda q, T: q.dma_start(T.mw[:, 0:V], T.am[:]), [R("mw", 0, V)], [], 2.6)
+    add("g", lambda g, T: [g.iota(T.ji[:], [[1, 128]], 0, 0)], [R("ji")], [], 0.4)
+    add("g", lambda g, T: [g.iota(T.pi[:, 0:1], [[0, 1]], 0, 1)], [R("pi", 0, 1)], [], 0.15)
+    ts(win(0, 0, G), R("xi", 0, G), -2048.0, A.add)
+    k0 = exchange(0, win(0, 0, G), win(0, V, W))
+    add("g", lambda g, T: [g.iota(T.tab[:], [[1, 1296]], 0, 0)], [R("tab")], [], 2.7, after=[k0])
+    exchange(NP, R("mw", 0, G), R("mw", V, W))
+    ts(win(0, G, V), R("xi", G, V), -2048.0, A.add)
+    cp(R("off", 0, 320), R("nbi"))
+    ts(R("nb16"), R("nbi"), -C0, A.add)
+
+    p0 = R("pi", 0, 1)
+    ts(R("pi", 1, 2), p0, 4, A.arith_shift_right)
+    ts(R("pi", 2, 3), p0, 15, A.bitwise_and)
+    ts(R("pi", 3, 4), p0, 2, A.arith_shift_right, 3, A.bitwise_and)
+    ts(R("pi", 4, 5), p0, 3, A.bitwise_and)
+    ts(R("pi", 5, 6), p0, 2, A.arith_shift_right)
+    cp(R("col", 0, 6), R("pi", 0, 6))
+    cp(R("jf"), R("ji"))
+    ts(R("i32m"), R("jf"), col(cP), A.is_equal)
+    ts(R("ti"), R("ji"), 4, A.arith_shift_right)
+    ts(R("jt", 0, 128), R("ti"), col(cG), A.is_equal)
+    blk, eye = R("jt", 0, 128), R("i32m")
+    ts(R("mq"), R("jf", 0, 16), col(cI), A.is_equal)
+    ts(R("mr"), R("jf", 0, 4), col(cR), A.is_equal)
+    cp(m16(I16), eye)
+    cp(mb(BLK), blk)
+    for q in range(16):
+        if q % 2:
+            ts(m16(SEL + q), mb(BLK), R("mq", q, q + 1), A.mult)
+        else:
+            act(m16(SEL + q), blk, AF.Copy, scale=R("mq", q, q + 1))
+    ms(R("nbw", 5120, 5376), -C0)
+    banks = ["L0", "L1", "L2", "T0", "T1"]
+    for q in range(16):
+        b = R(banks[q % 5], 0, 320)
+        mm([(b, m16(SEL + q), R("nb16"))])
+        if q % 2:
+            cp(R("nbw", 320 * q, 320 * q + 320), b)
+        else:
+            act(R("nbw", 320 * q, 320 * q + 320), b, AF.Copy)
+    for q in range(16):
+        ts(m16(DIAG + q), m16(I16), R("mq", q, q + 1), A.mult)
+    ms(R("ones"), 1.0)
+    act(m16(I16S), eye, AF.Copy, scale=0.0625)
+    for k, c in ((N64, -64.0), (N1024, -1024.0), (CMI, -15.0 / 32), (MI, M), (NMI, -M), (IB, 1.0)):
+        act(mb(k), eye, AF.Copy, scale=c)
+    for k, (lo, hi) in enumerate(CH):
+        act(R("x16", lo, hi), win(0, lo, hi), AF.Copy)
+    act(m16(NI16), eye, AF.Copy, scale=-1.0)
+    red(col(cFA), R("mq", 4, 7))
+    red(col(12), R("mq", 7, 9))
+    red(col(13), R("mq", 9, 12))
+    red(col(14), R("mq", 5, 8, 2))
+    red(col(15), R("mq", 6, 9, 2))
+    ts(col(cFB), col(12), R("mq", 4, 5), A.subtract, R("mr", 3, 4), A.subtract)
+    ts(col(cFC), col(13), col(14), A.subtract, R("mr", 0, 1), A.subtract)
+    ts(col(cFD), col(15), col(13), A.add, -1.0, A.mult)
+    ts(col(cAD), R("mr", 0, 1), R("mr", 3, 4), A.add)
+    for r, c in enumerate((cFA, cFC, cFB, cFD)):
+        act(m16(CF + r), eye, AF.Copy, scale=col(c))
+    ts(m16(CW), m16(I16), R("mr", 0, 1), A.mult, -1.0, A.mult)
+    ts(m16(CW + 1), m16(I16), R("mr", 3, 4), A.mult, -1.0, A.mult)
+    ts(R("ti"), R("ji"), 2, A.arith_shift_right)
+    ts(R("tb"), R("ti"), col(cQ4), A.is_equal)
+    ts(R("tw"), R("jf"), col(cP), A.is_gt)
+    tt(mb(LTRI), R("tb"), R("tw"), A.mult)
+    act(mb(WAD), blk, AF.Copy, scale=col(cAD))
+    act(mb(BM4), blk, AF.Copy, scale=-4.0)
+    ts(col(cTQ), col(cT), 80.0, A.mult, 1.0, A.add)
+    ts(mb(WPA), mb(BLK), col(cTQ), A.mult, R("mr", 0, 1), A.mult)
+    ts(mb(WPD), mb(BLK), col(cTQ), A.mult, R("mr", 3, 4), A.mult)
+    ts(R("spare"), R("jf", 0, 16), 16.0, A.mult, col(cI), A.add)
+    ln2 = math.log(2.0)
+    ts(R("vt", 0, 4), R("spare", 0, 4), -2 * ln2, A.mult, 64 * ln2, A.add)
+    act(R("w4"), R("vt", 0, 4), AF.Exp, extra=1.3)
+    ts(R("thg"), R("jf", 0, 64), -2 * ln2, A.mult, 64 * ln2 + math.log(6.5), A.add)
+    act(R("thr"), R("thg"), AF.Exp)
+    ts(R("spare"), R("spare"), 5120.0, A.add)
+    cp(R("lu"), R("l32"))
+    cp(R("lf"), R("l32"))
+    cp(R("rep", 0, 128), IND(R("tab"), R("lu", 0, 8)))
+    cp(R("rep", 128, 256), IND(R("tab", 0, 32), R("lu", 24, 32)))
+    ts(R("lq16"), R("lf", 16, 24), 0.25, A.mult)
+    ts(R("ti", 0, 8), R("l32", 0, 8), 4, A.arith_shift_right)
+    ts(R("tw", 0, 8), R("ti", 0, 8), -5119.0, A.mult)
+    ts(R("tb", 0, 8), R("lf", 0, 8), 320.0, A.mult)
+    tt(R("to", 0, 8), R("tb", 0, 8), R("tw", 0, 8), A.add)
+    ts(R("tw", 0, 8), R("lf", 8, 16), 80.0, A.mult)
+    ts(R("tw", 8, 16), R("lf", 32, 40), 80.0, A.mult)
+    for t in range(2):
+        for h in range(2):
+            tt(R("o1f", 8 * t + 4 * h, 8 * t + 4 * h + 4), R("to", 4 * t, 4 * t + 4), R("tw", 8 * h + 4 * t, 8 * h + 4 * t + 4), A.add)
+        ts(R("at16", 256 * t + 128, 256 * t + 192), R("rep", 64 * t, 64 * t + 64), -C0, A.add)
+    cp(R("o1"), R("o1f"))
+    ts(R("vt"), R("lf", 8, 24), -80.0, A.mult)
+    for t in range(2):
+        cp(R("pt", 16 * t, 16 * t + 4), R("spare", 0, 4))
+        cp(R("pt", 16 * t + 12, 16 * t + 16), R("spare", 0, 4))
+        tt(R("pt", 16 * t + 4, 16 * t + 8), R("vt", 8 + 4 * t, 12 + 4 * t), R("spare", 0, 4), A.add)
+        tt(R("pt", 16 * t + 8, 16 * t + 12), R("vt", 4 * t, 4 * t + 4), R("spare", 0, 4), A.add)
+
+    HI0, B0 = C0 / 16 - 0.4921875, 320.0 * C0
+
+    def place(v, n, at):
+        ts(R("ti", at, at + n), v, 0.0625, A.mult, HI0, A.add)
+        ts(R("tb", at, at + n), v, 320.0, A.mult, B0, A.add)
+
+    def place_sum(out, n, at):
+        ts(R("tw", at, at + n), R("ti", at, at + n), -5119.0, A.mult)
+        tt(out, R("tw", at, at + n), R("tb", at, at + n), A.add)
+
+    nbw = R("nbw")
+
+    def names(h):
+        act1(R("nm16", 0, 512), IND(nbw, R("o2", 0, 32)), AF.Copy)
+        if h:
+            act(R("nm16", 512, 1024), IND(nbw, R("o2", 32, 64)), AF.Copy)
+        else:
+            cp1(R("nm16", 512, 1024), IND(nbw, R("o2", 32, 64)))
+
+    def names_list(h):
+        mm(diag(R("L1", 256, 320), "nm16", 0, 1024))
+        ts(R("o4", 64 * h, 64 * h + 64), R("L1", 256, 320), C0, A.add)
+
+    def switch(flag, h, t, dst):
+        mm(diag(R("L2", 480, 484), "wn16", flag, flag + 64))
+        for c in range(4):
+            ts(R("osc", 16 * h + c, 16 * h + 16, 4), R("dn", c, 16, 4), R("L2", 480 + c, 481 + c), A.mult, R("spare", c, c + 1), A.add)
+        for k, u in enumerate((2, 3, 0, 1) if h else (1, 0, 3, 2)):
+            cp(IND(nbw, R("osc", 16 * h + 4 * u, 16 * h + 4 * u + 4)), R("at16", 256 * t + 64 * k, 256 * t + 64 * k + 64))
+        dma(lambda q, T: q.dma_start(T.off32[:], T.nbw[0:128:18, 0:5120]), [R("off32")], [R("nbw", 0, 5120)], 2.8)
+        ts(R("off", 320 * dst, 320 * dst + 320), R("off32"), C0, A.add)
+
+    def lanes(t, dst):
+        a0 = 256 * t
+
+        def at(r):
+            return R("at16", a0 + 64 * r, a0 + 64 * r + 64)
+        cp(R("at16", a0, a0 + 128), IND(nbw, R("o1", 8 * t, 8 * t + 8)))
+        pl = R("L2", 0, 4)
+        mm(diag(pl, "at16", a0 + 64, a0 + 128) + [(pl, m16(I16), R("lq16", 4 * t, 4 * t + 4))])
+        place(pl, 4, 64)
+        for c in range(4):
+            ts(R("oc", c, c + 1), R("ti", 64 + c, 65 + c), -5119.0, A.mult, R("tb", 64 + c, 65 + c), A.add)
+        cp(at(3), IND(nbw, R("oc")))
+        pc = R("L2", 64, 80)
+        mm(diag(pc, "at16", a0, a0 + 256))
+        place(pc, 16, 0)
+        cp(R("al"), pc)
+        place_sum(R("to", 0, 16), 16, 0)
+        for p in range(4):
+            ts(R("o2", 16 * p, 16 * p + 16), R("to", 0, 16), 80.0 * p, A.add)
+        ts(R("eg"), R("at16", a0, a0 + 256), -128.0, A.is_ge)
+        ts(R("o3"), R("al"), C0, A.add)
+        names(0)
+        tt(R("dn"), R("to", 0, 16), R("pt", 16 * t, 16 * t + 16), A.subtract)
+        uf, uw, n2 = R("L0", 0, 64), R("L0", 64, 128), R("L2", 128, 192)
+        ad = [(i, R("nm16", 64 * (4 * (i % 4) + i // 4), 64 * (4 * (i % 4) + i // 4 + 1))) for i in (0, 1, 2, 3, 12, 13, 14, 15)]
+        mm([(uf, m16(CF + r), at(r)) for r in range(4)] + [(uw, m16(CW), at(2)), (uw, m16(CW + 1), at(1))])
+        act(R("tm"), R("L0", 0, 128), AF.Copy, scale=-1.0)
+        mm([(n2, m16(DIAG + i), u) for i, u in ad])
+        tt(R("eb", 64, 128), n2, R("tm", 64, 128), A.is_equal)
+        tt(R("eb", 0, 64), n2, R("tm", 0, 64), A.is_equal)
+        mm([(R("L2", 256, 320), mb(LTRI), R("eb", 64, 128))])
+        chg = R("eb", 128, 192)
+        tt(chg, R("eb", 64, 128), R("L2", 256, 320), A.is_gt)
+        sc = R("L2", 0, 64)
+        mm([(sc, mb(N64), R("eg", 64 * r, 64 * r + 64)) for r in (0, 1, 3)] + [(sc, mb(BM4), R("eb", 0, 64)), (sc, mb(WAD), chg),
+            (R("L2", 64, 128), mb(WPA), chg), (R("L2", 128, 192), mb(WPD), chg)])
+        ts(R("gp16"), R("L2", 0, 192), -1.0, A.add, 0.0, A.max)
+        for r in range(4):
+            for c in range(4):
+                k = 4 * c + r
+                ts(R("eq", 256 * k, 256 * k + 256), R("at16", a0, a0 + 256), R("al", 4 * r + c, 4 * r + c + 1), A.is_equal)
+        for c in range(4):
+            mm([(R("L1", 64 * c, 64 * c + 64), mb(IB), R("eq", 1024 * c + 64 * k, 1024 * c + 64 * k + 64)) for k in range(16)])
+        act(R("sb"), R("L1", 0, 256), AF.Copy)
+        names_list(0)
+        mm(diag(R("L2", 320, 332), "gp16", 0, 192))
+        for c in range(4):
+            ts(mb(LW + c), mb(BLK), R("L2", 320 + c, 321 + c), A.mult, R("w4", c, c + 1), A.mult)
+        tt(R("dn", 0, 4), R("L2", 324, 328), R("dn", 0, 4), A.add)
+        tt(R("dn", 12, 16), R("L2", 328, 332), R("dn", 12, 16), A.add)
+        mm([(R("L2", 384, 448), mb(LW + c), R("sb", 64 * c, 64 * c + 64)) for c in range(4)])
+        tt(R("thg"), R("thr"), R("gp16", 0, 64), A.mult)
+        tt(R("wn16", 0, 64), R("L2", 384, 448), R("thg"), A.is_lt)
+        switch(0, 0, t, dst)
+        ts(R("hqw", 0, 64), R("wn16", 0, 64), -99.0, A.mult, 99.0, A.add)
+        tt(R("hqw", 64, 128), R("hqw", 0, 64), R("rep", 128 + 64 * t, 192 + 64 * t), A.add)
+
+    def stress(s, h):
+        act(R("xo"), IND(win(s), R("o3")), AF.Copy)
+        for u in range(2):
+            a, b = 512 * u, 512 * u + 512
+            act(R("ld", a, b), IND(win(s), R("o4", 64 * h + 32 * u, 64 * h + 32 * u + 32)), AF.Copy)
+            bk = "L%d" % u
+            for v in range(2):
+                o = R(bk, 256 * v, 256 * v + 256)
+                mm([(o, m16(I16), R("ld", a + 256 * v, a + 256 * v + 256)), (o, m16(NI16), R("xo"))])
+            ts(R("lc", a, b), R(bk), -2047.0, A.max, 2047.0, A.min)
+            if h:
+                ts(R("ls", a, b), R("lc", a, b), -1.0, A.max, 1.0, A.min)
+            else:
+                act(R("ls", a, b), R("lc", a, b), AF.Sign)
+            mm([(R(bk), m16(I16), R("lc", a, b)), (R(bk), mb(N1024), R("ls", a, b))])
+            act(R("sq", a, b), R(bk), AF.Square)
+        for u in range(2):
+            mm([(R("L0", 0, 64), R("i32m"), R("sq", 512 * u + 64 * v, 512 * u + 64 * v + 64)) for v in range(8)], first=u == 0, last=u == 1)
+        if h == 0:
+            act(R("sf"), R("L0", 0, 64), AF.Copy)
+
+    def votes(t, dst):
+        tt(R("wb"), R("L0", 0, 64), R("sf"), A.is_gt)
+        mm([(R("L2", 384, 448), mb(BLK), R("wb"))])
+        tt(R("wn16", 64, 128), R("L2", 384, 448), R("hqw", 64, 128), A.is_ge)
+        switch(64, 1, t, dst)
+
+    turn = [0, 0]
+
+    def diffs(s, k, o, nact):
+        lo, hi, bank = k
+        m = hi - lo
+        b = turn[0] % NSET
+        turn[0] += 1
+
+        def sl(name, p, n=1):
+            return R(name, 4 * CM * b + m * p, 4 * CM * b + m * (p + n))
+
+        def offs(p):
+            return IND(win(s), R("off", 320 * o + 80 * p + lo // 16, 320 * o + 80 * p + hi // 16))
+        for p in range(4 - nact, 4):
+            xk = R("X%d" % (turn[1] % 3), 0, m)
+            turn[1] += 1
+            act1(sl("d16", p), offs(p), AF.Copy)
+            mm([(xk, m16(NI16), R("x16", V * (s % 2) + lo, V * (s % 2) + hi)), (xk, m16(I16), sl("d16", p))])
+            ts(sl("c16", p), xk, -2047.0, A.max, 2047.0, A.min)
+        for p in range(4 - nact):
+            tt(sl("d16", p), offs(p), R("x16", V * (s % 2) + lo, V * (s % 2) + hi), A.subtract)
+        one = s == NP - 1
+        for p, n in ((0, 1), (1, 1), (2, 1)) if one else ((0, 2),):
+            ts(sl("c16", p, n), sl("d16", p, n), -2047.0, A.max, 2047.0, A.min)
+        for p, n in ((0, 1), (1, 1), (2, 1), (3, 1)) if one else (((0, 2), (2, 1), (3, 1)) if lo == 0 else ((0, 2), (2, 2))):
+            src = sl("d16" if p < 4 - nact else "c16", p, n)
+            if p == 2 and bank in (SIGNF if one else SIGNV):
+                ts(sl("s16", p, n), src, -1.0, A.max, 1.0, A.min)
+            else:
+                act(sl("s16", p, n), src, AF.Sign)
+        return b, sl
+
+    def sweep(s, o):
+        xa, xb = V * (s % 2), V * ((s + 1) % 2)
+        for k in SUB:
+            lo, hi, bank = k
+            boost[0] = -LATER * lo / V
+            m = hi - lo
+            tb = R("T%d" % (turn[0] % 2), 0, m)
+            mm([(tb, m16(I16), R("x16", xa + lo, xa + hi)), (tb, mb(CMI), R("ones", 0, m))], last=False)
+            b, sl = diffs(s, k, o, 2)
+            for kind, p in ("c0", "c1", "s0", "s1", "c2", "s2", "c3", "s3") if lo == 0 else ("c0", "c1", "s0", "s1", "c2", "c3", "s2", "s3"):
+                end = kind + p == "s3"
+                mm([(tb, m16(I16S) if kind == "c" else mb(N64), sl(kind + "16", int(p)))] + ([(tb, mb(MI), R("ones", 0, m)), (tb, mb(NMI), R("ones", 0, m))] if end else []),
+                   first=False, last=end)
+            ts(win(s + 1, lo, hi), tb, -2048.0, A.max, 2047.0, A.min)
+            if lo == 0:
+                exchange(s + 1, win(s + 1, 0, G), win(s + 1, V, W))
+            if hi == CH[bank][1]:
+                lo = CH[bank][0]
+                act(R("x16", xb + lo, xb + hi), win(s + 1, lo, hi), AF.Copy)
+        boost[0] = 0.0
+
+    def final(s, o):
+        nf = 0
+        for k in FSUB:
+            lo, hi, bank = k
+            boost[0] = -LATEF * lo / V
+            m = hi - lo
+            yb = R("T%d" % (turn[0] % 2), 0, m)
+            b, sl = diffs(s, k, o, 1)
+            for p in (3, 0, 1, 2):
+                fb = R("L%d" % (nf % 3), 0, m)
+                e = win(0, CM * (nf % 4), CM * (nf % 4) + m)
+                tq = win(1, CM * (nf % 4), CM * (nf % 4) + m)
+                nf += 1
+                mm([(fb, m16(I16), sl("c16", p)), (fb, mb(N1024), sl("s16", p))])
+                act(e, fb, AF.Square)
+                act(e, e, AF.Exp, scale=-2.0 ** -19)
+                tt(tq, IND(R("mw"), R("off", 320 * o + 80 * p + lo // 16, 320 * o + 80 * p + hi // 16)), e, A.mult)
+                mm([(yb, R("i32m"), tq)], first=p == 3, last=p == 2)
+            cp(win(2, lo, hi), yb)
+            dma(lambda q, T, lo=lo, hi=hi: q.dma_start(T.y[:, lo:hi], T.win[:, 2 * W + lo:2 * W + hi]), [], [win(2, lo, hi)])
+
+    for t in range(2):
+        lanes(t, 2 * t + 1)
+        stress(3 * t, 0)
+        names(1)
+        names_list(1)
+        sweep(3 * t, 2 * t)
+        sweep(3 * t + 1, 2 * t + 1)
+        stress(3 * t + 2, 1)
+        votes(t, 2 * t + 2)
+        sweep(3 * t + 2, 2 * t + 1)
+    final(6, 4)
+    return ops
+
+
+def schedule(ops):
+    hist = {}
+    for i, o in enumerate(ops):
+        deps = set(o["after"])
+        acc = [(r, True) for r in o["w"]] + [(r, False) for r in o["r"]]
+        for r, wr in acc:
+            ps = _ps(r)
+            for j, lo, hi, w2, st in hist.get(r[0], []):
+                if ps:
+                    if wr or w2 or ops[j]["eng"] != o["eng"] or "alt" in o or "alt" in ops[j]:
+                        deps.add(j)
+                elif (wr or w2) and lo < r[2] and r[1] < hi and not (st == r[3] > 1 and (lo - r[1]) % st):
+                    deps.add(j)
+        for r, wr in acc:
+            h = hist.setdefault(r[0], [])
+            if wr and (r[3] == 1 or _ps(r)):
+                h[:] = [] if _ps(r) else [e for e in h if not (r[1] <= e[1] and e[2] <= r[2])]
+        for r, wr in acc:
+            hist[r[0]].append((i, r[1], r[2], wr, r[3]))
+        deps.discard(i)
+        o["deps"] = sorted(deps)
+    n = len(ops)
+
+    def lat(j, i):
+        a, b = ops[j]["eng"], ops[i]["eng"]
+        return 0.0 if a == b == "t" or b == "x" else (0.06 if a == b else 0.12)
+    succ = [[] for _ in range(n)]
+    for i, o in enumerate(ops):
+        for j in o["deps"]:
+            succ[j].append(i)
+    prio = [0.0] * n
+    for i in range(n - 1, -1, -1):
+        prio[i] = ops[i]["cost"] + max([prio[k] + lat(i, k) + HOP for k in succ[i]] + [0.0])
+    prio = [p + o["boost"] for p, o in zip(prio, ops)]
+    left = [len(o["deps"]) for o in ops]
+    ready = {i: 0.0 for i in range(n) if not left[i]}
+    free = {e: 0.0 for e in "vatgsx"}
+    order = {e: [] for e in "vatgsx"}
+    end = [0.0] * n
+    seq = []
+    while ready:
+        best = min(max(t, free[ops[i]["eng"]]) for i, t in ready.items())
+        take = [i for i, t in ready.items() if "alt" in ops[i] and max(t, free[ops[i]["alt"][0]]) < best
+                and max(t, free[ops[i]["alt"][0]]) + ops[i]["alt"][2] < max(t, free[ops[i]["eng"]]) + ops[i]["cost"] + STEAL
+                and not any(ops[c]["eng"] == ops[i]["alt"][0] and u < max(t, free[ops[c]["eng"]]) + IDLE for c, u in ready.items())]
+        if take:
+            o = ops[max(take, key=lambda c: (prio[c], -c))]
+            o["eng"], o["fn"], o["cost"] = o.pop("alt")
+            continue
+        cand = [i for i, t in ready.items() if max(t, free[ops[i]["eng"]]) <= best + 0.04]
+        e = ops[min(cand, key=lambda i: (max(ready[i], free[ops[i]["eng"]]), i))]["eng"]
+        i = max([c for c in cand if ops[c]["eng"] == e], key=lambda c: (prio[c], -c))
+        soon = [c for c, t in ready.items() if ops[c]["eng"] == e and t <= best + min(LOOK, ops[i]["cost"]) and prio[c] > prio[i] + GAP]
+        if soon:
+            i = max(soon, key=lambda c: (prio[c], -c))
+        st = max(ready.pop(i), free[e])
+        end[i] = st + ops[i]["cost"]
+        ops[i]["start"] = st
+        free[e] = st + 0.06 if e == "s" else (0.0 if e == "x" else end[i])
+        order[e].append(i)
+        seq.append(i)
+        for k in succ[i]:
+            left[k] -= 1
+            if not left[k]:
+                ready[k] = max(end[j] + lat(j, k) for j in ops[k]["deps"])
+
+    def pack(keys, before, back):
+        slots = {e: [] for e in "vatg"}
+        fin = [0.0] * n
+        for i in sorted(range(n), key=lambda i: keys[i]):
+            e, c = ops[i]["eng"], ops[i]["cost"]
+            st = max([fin[j] + (lat(i, j) if back else lat(j, i)) for j in before[i]] + [0.0])
+            if e in slots:
+                sl = slots[e]
+                at = len(sl)
+                while at and sl[at - 1][1] > st:
+                    at -= 1
+                while at < len(sl) and st + c > sl[at][0] + 1e-9:
+                    st = max(st, sl[at][1])
+                    at += 1
+                sl.insert(at, (st, st + c))
+            fin[i] = st + c
+        return fin
+    for _ in range(PASSES):
+        fin = pack([(-round(end[i], 6), -i) for i in range(n)], succ, True)
+        end = pack([(-round(fin[i], 6), i) for i in range(n)], [o["deps"] for o in ops], False)
+    for i, o in enumerate(ops):
+        o["start"] = end[i] - o["cost"]
+    seq = sorted(range(n), key=lambda i: (round(ops[i]["start"], 6), i))
+    order = {e: [i for i in seq if ops[i]["eng"] == e] for e in "vatgsx"}
+    count = {e: 0 for e in "vatg"}
+    known = {e: {} for e in "vatgs"}
+    clock = [None] * n
+    for i in seq:
+        o = ops[i]
+        e = o["eng"]
+        if e == "x":
+            o["tag"] = (o["sem"], 32)
+            clock[i] = {o["sem"]: 32}
+            continue
+        kn = known[e]
+        waits = []
+        for j in sorted(o["deps"], key=lambda j: -end[j]):
+            d = ops[j]
+            if d["tag"] is None or (e == "t" and d["eng"] == "t"):
+                continue
+            s, c = d["tag"]
+            if kn.get(s, 0) < c:
+                waits.append((s, c))
+                for s2, c2 in clock[j].items():
+                    kn[s2] = max(kn.get(s2, 0), c2)
+        o["waits"] = waits
+        if e == "s":
+            o["tag"] = (o["sem"], 16)
+        elif o["ninc"]:
+            count[e] += o["ninc"]
+            o["tag"] = ("q" + e, count[e])
+        else:
+            o["tag"] = None
+        clock[i] = dict(kn)
+        if o["tag"]:
+            clock[i][o["tag"][0]] = o["tag"][1]
+    return order, count, max(end)
+
+
+OPS = build()
+ORDER, COUNT, SPAN = schedule(OPS)
+
+
+def _mask(engs):
+    return sum(1 << e for e in engs)
+
+
+def helpers(core, T, topo):
+    r = T.rank_of(core)
+    dsts = [T.cores[(r + d) % len(T.cores)] for d in DS]
+    hs = [c for c in topo.cores_of(core) if c != core and all(topo.may_write(c, d) for d in dsts)]
+    hs.sort(key=lambda c: (topo.die(c) != topo.die(core), c))
+    return hs[:4], dsts
+
+
+def _slot(T, s, row):
+    return T.hopm[row:row + 128, :] if s == NP else T.hop[256 * s + row:256 * s + row + 128, :]
+
+
+def _cols(T, s, lo):
+    return T.mw[:, lo:lo + H] if s == NP else T.win[:, s * W + lo:s * W + lo + H]
+
+
+def helper_program(g, core, owner, T, topo):
+    hs, dsts = helpers(owner, T, topo)
+    k = hs.index(core)
+    half, total = k // 2, 0
+    for s in [0, NP] + list(range(1, NP)):
+        g.wait_ge(T.sem["rel%d" % s], 8)
+        trs = []
+        for u in range(2):
+            b = 2 * (k % 2) + u
+            rid, pid = topo.addr(dsts[b], core)
+            engs = topo.engines(core, dsts[b])
+            trs.append(RemoteDMATransfer(dst_ids=[DstId(rid=rid, pnc=pid)], dma_engine_mask=_mask(engs[4 * u:4 * u + 4]),
+                                         remote_sem=T.sem["arr%d" % s], src=_slot(T, s, 16 * b),
+                                         dst=_cols(T, s, V + G * b + H * half)))
+        g.remote_dma_fused(trs, local_sem=T.sem.sent)
+        total += 8
+    g.wait_ge(T.sem.sent, total)
+
+
+def rank_program(g, core, T, topo):
+    if T.rank_of(core) is None:
+        for owner in topo.cores_of(core):
+            if T.rank_of(owner) is not None and core in helpers(owner, T, topo)[0]:
+                helper_program(g, core, owner, T, topo)
+        return
+    hs, _ = helpers(core, T, topo)
+    queue = {"v": g.vector, "a": g.scalar, "t": g.tensor, "g": g, "s": g.sync}
+    sent = 0
+    for e in "svatg":
+        q = queue[e]
+        for i in ORDER[e]:
+            o = OPS[i]
+            for s, c in o["waits"]:
+                q.wait_ge(T.sem[s], c)
+            if e == "s":
+                o["fn"](q, T).then_inc(T.sem[o["sem"]], 16)
+            elif isinstance(o["fn"], tuple):
+                s = o["fn"][1]
+                trs = []
+                for k, h in enumerate(hs):
+                    rid, pid = topo.addr(h, core)
+                    engs = topo.engines(core, h)
+                    trs.append(RemoteDMATransfer(dst_ids=[DstId(rid=rid, pnc=pid)] * 2, dma_engine_mask=_mask(engs[4 * k:4 * k + 4]),
+                                                 remote_sem=T.sem["rel%d" % s], srcs=[_cols(T, s, H * (k // 2))],
+                                                 dsts=[_slot(T, s, 0), _slot(T, s, 128)]))
+                g.remote_dma_fused(trs, local_sem=T.sem.sent)
+                sent += 16
+            else:
+                for ins in o["fn"](g, T):
+                    ins.then_inc(T.sem["q" + e], 1)
+    for e in "vatg":
+        g.wait_ge(T.sem["q" + e], COUNT[e])
+    for i in ORDER["s"] + ORDER["x"]:
+        g.wait_ge(T.sem[OPS[i]["tag"][0]], OPS[i]["tag"][1])
+    g.wait_ge(T.sem.sent, sent)

@@ -8,7 +8,7 @@ H = G // 2
 M = 12582912.0
 C0 = 1408.0
 CH = [(0, 384), (384, 832), (832, 1280)]
-CM, NSET = 448, 3
+CM, NSET = 448, 2
 NP = 7
 F32, F16, B16, I32, U16 = "float32", "float16", "bfloat16", "int32", "uint16"
 
@@ -18,7 +18,7 @@ def _sb(n, dt):
 
 
 SCRATCH = {
-    "win": _sb(NP * W, F32), "mw": _sb(W, B16), "nbw": _sb(5376, F32), "xi": _sb(V, I32), "x16": _sb(2 * V, F16),
+    "win": _sb(NP * W, F32), "mw": _sb(W, B16), "nbw": _sb(5376, F32), "xi": _sb(V, I32), "x16": _sb(NP * V, F16),
     "nbi": _sb(320, I32), "nb16": _sb(320, F16), "off": _sb(5 * 320, U16), "off32": _sb(320, F32),
     "d16": _sb(4 * NSET * CM, F16), "c16": _sb(4 * NSET * CM, F16), "s16": _sb(4 * NSET * CM, B16),
     "m16": _sb(41 * 128, F16), "mb": _sb(16 * 128, B16), "i32m": _sb(128, F32), "ones": _sb(CM, B16),
@@ -44,12 +44,14 @@ SEMAPHORES = (["qv", "qa", "qt", "qg", "sent"] + ["arr%d" % s for s in range(NP 
 A = AluOpType
 AF = ActivationFunctionType
 CYC, PEC = 1.0e-3, 0.5e-3
-XLAT = 7.0
-HOP, LOOK, GAP, STEAL, IDLE = 0.15, 0.3, 2.0, 0.2, 0.15
-SUB = [(0, 384, 0), (384, 832, 1), (832, 1280, 2)]
-FSUB = [(0, 384, 0), (384, 832, 1), (832, 1152, 2), (1152, 1280, 2)]
-SIGNV, SIGNF = (), (1, 2)
-PASSES, LATER, LATEF = 2, 6.0, 3.0
+XLAT, GATHER = 10.0, 1.56
+SAME, CROSS, NOISE, SEED = 0.12, 0.25, 0.0, 1.0
+MORE, MOREF, LSV = (), (384,), 2
+HOP, LOOK, GAP, STEAL, IDLE = 0.0, 0.3, 2.0, {"v": 0.3, "a": 0.3}, 0.3
+SUB = [(0, 384, 0), (384, 832, 1), (832, 1152, 2), (1152, 1280, 2)]
+FSUB = [(0, 384, 0), (384, 832, 1), (832, 1088, 2), (1088, 1280, 2)]
+SIGNV, SIGNF = (), (1,)
+PASSES, LATER, LATEF = 2, 0.0, 0.0
 
 
 def R(name, lo=0, hi=None, st=1):
@@ -105,7 +107,7 @@ def build():
         if out[0] == "*":
             return 0.05 + 3.8 * n * CYC
         if ins[0][0] == "*":
-            return 0.05 + 1.56 * n * CYC
+            return 0.05 + GATHER * n * CYC
         return 0.02 + max(64, base * n) * CYC
 
     def ts(out, a, s1, o0, s2=None, o1=None):
@@ -141,7 +143,7 @@ def build():
             if scale is not None:
                 kw["scale"] = _ap(T, scale)
             return [g.scalar.activation(_ap(T, out), _ap(T, a), f, **kw)]
-        return add("a", fn, [out], [a, bias, scale], 0.065 + extra + max(64, _n(out) * (1.56 if a[0] == "*" else 1)) * CYC)
+        return add("a", fn, [out], [a, bias, scale], 0.065 + extra + max(64, _n(out) * (GATHER if a[0] == "*" else 1)) * CYC)
 
     ts1, cp1, act1 = ts, cp, act
 
@@ -268,7 +270,7 @@ def build():
     act(m16(I16S), eye, AF.Copy, scale=0.0625)
     for k, c in ((N64, -64.0), (N1024, -1024.0), (CMI, -15.0 / 32), (MI, M), (NMI, -M), (IB, 1.0)):
         act(mb(k), eye, AF.Copy, scale=c)
-    for k, (lo, hi) in enumerate(CH):
+    for lo, hi in CH:
         act(R("x16", lo, hi), win(0, lo, hi), AF.Copy)
     act(m16(NI16), eye, AF.Copy, scale=-1.0)
     red(col(cFA), R("mq", 4, 7))
@@ -422,7 +424,7 @@ def build():
                 o = R(bk, 256 * v, 256 * v + 256)
                 mm([(o, m16(I16), R("ld", a + 256 * v, a + 256 * v + 256)), (o, m16(NI16), R("xo"))])
             ts(R("lc", a, b), R(bk), -2047.0, A.max, 2047.0, A.min)
-            if h:
+            if h and u < LSV:
                 ts(R("ls", a, b), R("lc", a, b), -1.0, A.max, 1.0, A.min)
             else:
                 act(R("ls", a, b), R("lc", a, b), AF.Sign)
@@ -456,15 +458,15 @@ def build():
             xk = R("X%d" % (turn[1] % 3), 0, m)
             turn[1] += 1
             act1(sl("d16", p), offs(p), AF.Copy)
-            mm([(xk, m16(NI16), R("x16", V * (s % 2) + lo, V * (s % 2) + hi)), (xk, m16(I16), sl("d16", p))])
+            mm([(xk, m16(NI16), R("x16", V * s + lo, V * s + hi)), (xk, m16(I16), sl("d16", p))])
             ts(sl("c16", p), xk, -2047.0, A.max, 2047.0, A.min)
         for p in range(4 - nact):
-            tt(sl("d16", p), offs(p), R("x16", V * (s % 2) + lo, V * (s % 2) + hi), A.subtract)
+            tt(sl("d16", p), offs(p), R("x16", V * s + lo, V * s + hi), A.subtract)
         one = s == NP - 1
-        for p, n in ((0, 1), (1, 1), (2, 1)) if one else ((0, 2),):
+        for p, n in [(p, 1) for p in range(4 - nact)] if one else ((0, 4 - nact),):
             ts(sl("c16", p, n), sl("d16", p, n), -2047.0, A.max, 2047.0, A.min)
         for p, n in ((0, 1), (1, 1), (2, 1), (3, 1)) if one else (((0, 2), (2, 1), (3, 1)) if lo == 0 else ((0, 2), (2, 2))):
-            src = sl("d16" if p < 4 - nact else "c16", p, n)
+            src = sl("d16" if p + n <= 4 - nact else "c16", p, n)
             if p == 2 and bank in (SIGNF if one else SIGNV):
                 ts(sl("s16", p, n), src, -1.0, A.max, 1.0, A.min)
             else:
@@ -472,14 +474,14 @@ def build():
         return b, sl
 
     def sweep(s, o):
-        xa, xb = V * (s % 2), V * ((s + 1) % 2)
+        xa, xb = V * s, V * (s + 1)
         for k in SUB:
             lo, hi, bank = k
             boost[0] = -LATER * lo / V
             m = hi - lo
             tb = R("T%d" % (turn[0] % 2), 0, m)
             mm([(tb, m16(I16), R("x16", xa + lo, xa + hi)), (tb, mb(CMI), R("ones", 0, m))], last=False)
-            b, sl = diffs(s, k, o, 2)
+            b, sl = diffs(s, k, o, 3 if lo in MORE else 2)
             for kind, p in ("c0", "c1", "s0", "s1", "c2", "s2", "c3", "s3") if lo == 0 else ("c0", "c1", "s0", "s1", "c2", "c3", "s2", "s3"):
                 end = kind + p == "s3"
                 mm([(tb, m16(I16S) if kind == "c" else mb(N64), sl(kind + "16", int(p)))] + ([(tb, mb(MI), R("ones", 0, m)), (tb, mb(NMI), R("ones", 0, m))] if end else []),
@@ -499,7 +501,7 @@ def build():
             boost[0] = -LATEF * lo / V
             m = hi - lo
             yb = R("T%d" % (turn[0] % 2), 0, m)
-            b, sl = diffs(s, k, o, 1)
+            b, sl = diffs(s, k, o, 2 if lo in MOREF else 1)
             for p in (3, 0, 1, 2):
                 fb = R("L%d" % (nf % 3), 0, m)
                 e = win(0, CM * (nf % 4), CM * (nf % 4) + m)
@@ -509,8 +511,9 @@ def build():
                 act(e, fb, AF.Square)
                 act(e, e, AF.Exp, scale=-2.0 ** -19)
                 tt(tq, IND(R("mw"), R("off", 320 * o + 80 * p + lo // 16, 320 * o + 80 * p + hi // 16)), e, A.mult)
-                mm([(yb, R("i32m"), tq)], first=p == 3, last=p == 2)
-            cp(win(2, lo, hi), yb)
+                if p != 2:
+                    mm([(yb, R("i32m"), tq)], first=p == 3, last=p == 1)
+            tt(win(2, lo, hi), yb, tq, A.add)
             dma(lambda q, T, lo=lo, hi=hi: q.dma_start(T.y[:, lo:hi], T.win[:, 2 * W + lo:2 * W + hi]), [], [win(2, lo, hi)])
 
     for t in range(2):
@@ -552,7 +555,7 @@ def schedule(ops):
 
     def lat(j, i):
         a, b = ops[j]["eng"], ops[i]["eng"]
-        return 0.0 if a == b == "t" or b == "x" else (0.06 if a == b else 0.12)
+        return 0.0 if a == b == "t" or b == "x" else (SAME if a == b else CROSS)
     succ = [[] for _ in range(n)]
     for i, o in enumerate(ops):
         for j in o["deps"]:
@@ -560,7 +563,7 @@ def schedule(ops):
     prio = [0.0] * n
     for i in range(n - 1, -1, -1):
         prio[i] = ops[i]["cost"] + max([prio[k] + lat(i, k) + HOP for k in succ[i]] + [0.0])
-    prio = [p + o["boost"] for p, o in zip(prio, ops)]
+    prio = [p + o["boost"] + NOISE * math.sin(SEED * (i + 1.0) ** 1.1) for i, (p, o) in enumerate(zip(prio, ops))]
     left = [len(o["deps"]) for o in ops]
     ready = {i: 0.0 for i in range(n) if not left[i]}
     free = {e: 0.0 for e in "vatgsx"}
@@ -570,7 +573,7 @@ def schedule(ops):
     while ready:
         best = min(max(t, free[ops[i]["eng"]]) for i, t in ready.items())
         take = [i for i, t in ready.items() if "alt" in ops[i] and max(t, free[ops[i]["alt"][0]]) < best
-                and max(t, free[ops[i]["alt"][0]]) + ops[i]["alt"][2] < max(t, free[ops[i]["eng"]]) + ops[i]["cost"] + STEAL
+                and max(t, free[ops[i]["alt"][0]]) + ops[i]["alt"][2] < max(t, free[ops[i]["eng"]]) + ops[i]["cost"] + STEAL[ops[i]["alt"][0]]
                 and not any(ops[c]["eng"] == ops[i]["alt"][0] and u < max(t, free[ops[c]["eng"]]) + IDLE for c, u in ready.items())]
         if take:
             o = ops[max(take, key=lambda c: (prio[c], -c))]
@@ -679,7 +682,7 @@ def _cols(T, s, lo):
 def helper_program(g, core, owner, T, topo):
     hs, dsts = helpers(owner, T, topo)
     k = hs.index(core)
-    half, total = k // 2, 0
+    total = 0
     for s in [0, NP] + list(range(1, NP)):
         g.wait_ge(T.sem["rel%d" % s], 8)
         trs = []
@@ -689,7 +692,7 @@ def helper_program(g, core, owner, T, topo):
             engs = topo.engines(core, dsts[b])
             trs.append(RemoteDMATransfer(dst_ids=[DstId(rid=rid, pnc=pid)], dma_engine_mask=_mask(engs[4 * u:4 * u + 4]),
                                          remote_sem=T.sem["arr%d" % s], src=_slot(T, s, 16 * b),
-                                         dst=_cols(T, s, V + G * b + H * half)))
+                                         dst=_cols(T, s, V + G * b + H * (k // 2))))
         g.remote_dma_fused(trs, local_sem=T.sem.sent)
         total += 8
     g.wait_ge(T.sem.sent, total)

@@ -5,7 +5,7 @@ from concourse.mybir import AluOpType, AxisListType, ActivationFunctionType
 V, G, W = 1280, 384, 2816
 DS = [1, 2, 6, 7]
 H = G // 2
-M = 12582912.0
+CUT = [0, H, G]
 C0 = 1408.0
 CH = [(0, 384), (384, 832), (832, 1280)]
 CM, NSET = 448, 2
@@ -18,12 +18,13 @@ def _sb(n, dt):
 
 
 SCRATCH = {
-    "win": _sb(NP * W, F32), "mw": _sb(W, B16), "nbw": _sb(5376, F32), "xi": _sb(V, I32), "x16": _sb(NP * V, F16),
+    "win": _sb(NP * W, I32), "mw": _sb(W, B16), "nbw": _sb(5376, F32), "x16": _sb(NP * V, F16), "xi": _sb(V, I32),
+    "fe": _sb(4 * CM, F32), "fq": _sb(4 * CM, F32), "fy": _sb(V, F32), "e16": _sb(144, F16),
     "nbi": _sb(320, I32), "nb16": _sb(320, F16), "off": _sb(5 * 320, U16), "off32": _sb(320, F32),
     "d16": _sb(4 * NSET * CM, F16), "c16": _sb(4 * NSET * CM, F16), "s16": _sb(4 * NSET * CM, B16),
-    "m16": _sb(41 * 128, F16), "mb": _sb(16 * 128, B16), "i32m": _sb(128, F32), "ones": _sb(CM, B16),
-    "ji": _sb(128, I32), "jf": _sb(128, F32), "jt": _sb(256, F32), "pi": _sb(8, I32), "col": _sb(32, F32),
-    "mq": _sb(16, F32), "mr": _sb(4, F32), "tab": _sb(1296, I32),
+    "m16": _sb(25 * 128, F16), "mb": _sb(14 * 128, B16), "i32m": _sb(128, F32), "ones": _sb(CM, B16),
+    "ji": _sb(144, I32), "jf": _sb(144, F32), "jt": _sb(256, F32), "pi": _sb(8, I32), "col": _sb(32, F32),
+    "mq": _sb(16, F32), "mr": _sb(4, F32), "tab": _sb(V, I32), "fb16": _sb(144, B16),
     "l32": _sb(40, I32), "lu": _sb(40, U16), "lf": _sb(40, F32), "rep": _sb(256, F32),
     "lq16": _sb(8, F16), "w4": _sb(4, F32), "thr": _sb(64, F32), "spare": _sb(16, F32),
     "ti": _sb(128, I32), "tb": _sb(128, F32), "tw": _sb(128, F32), "to": _sb(128, F32),
@@ -31,27 +32,27 @@ SCRATCH = {
     "osc": _sb(32, U16), "at16": _sb(512, F16), "nm16": _sb(1024, F16), "eb": _sb(256, B16), "eg": _sb(256, B16),
     "gp16": _sb(192, F16), "eq": _sb(4096, B16), "sb": _sb(256, B16), "al": _sb(16, F32), "pt": _sb(32, F32),
     "vt": _sb(16, F32), "dn": _sb(16, F32), "tm": _sb(128, F32), "thg": _sb(64, F32),
-    "wn16": _sb(128, F16), "hqw": _sb(128, F32), "wb": _sb(64, B16),
+    "wn16": _sb(64, F16), "hqw": _sb(16, F32), "wb": _sb(64, B16),
     "xo": _sb(256, F16), "sq": _sb(1024, F32), "sf": _sb(64, F32),
     "ld": _sb(1024, F16), "lc": _sb(1024, F16), "ls": _sb(1024, B16),
-    "hop": ("dram", [NP * 256, H], F32), "hopm": ("dram", [256, H], B16),
+    "hop": ("dram", [NP * 256, H], I32), "hopm": ("dram", [256, H], B16),
 }
 for _n in ("X0", "X1", "X2", "T0", "T1", "L0", "L1", "L2"):
     SCRATCH[_n] = ("psum", [128, 512], F32)
 NDMA = 20
-SEMAPHORES = (["qv", "qa", "qt", "qg", "sent"] + ["arr%d" % s for s in range(NP + 1)] + ["rel%d" % s for s in range(NP + 1)]
+SEMAPHORES = (["qv", "qa", "qt", "qg", "sent"] + ["arr%d%s" % (s, h) for s in range(NP + 1) for h in "ab"] + ["rel%d" % s for s in range(NP + 1)]
               + ["dma%d" % k for k in range(NDMA)])
 A = AluOpType
 AF = ActivationFunctionType
 CYC, PEC = 1.0e-3, 0.5e-3
-XLAT, GATHER = 10.0, 1.56
-SAME, CROSS, NOISE, SEED = 0.12, 0.25, 0.0, 1.0
-MORE, MOREF, LSV = (), (384,), 2
-HOP, LOOK, GAP, STEAL, IDLE = 0.0, 0.3, 2.0, {"v": 0.3, "a": 0.3}, 0.3
-SUB = [(0, 384, 0), (384, 832, 1), (832, 1152, 2), (1152, 1280, 2)]
-FSUB = [(0, 384, 0), (384, 832, 1), (832, 1088, 2), (1088, 1280, 2)]
-SIGNV, SIGNF = (), (1,)
-PASSES, LATER, LATEF = 2, 0.0, 0.0
+XLAT, GATHER, SCATTER, SEND = 10.0, 1.56, 3.8, 0.6
+SAME, CROSS = 0.15, 0.3
+SUB0 = SUB1 = SUB2 = [(0, H, 2, (3,)), (H, G, 2, (3,)), (G, 832, 2, ()), (832, 1152, 2, ()), (1152, V, 2, ())]
+XHALF = (10.0, 8.5)
+ROUNDS, NOISE, FLIPS, TEMP, SEED = 1500, 0.3, 3, 0.3, 1
+NM0 = "a"
+FSUB = [(0, 448, 3, (0, 1, 2, 3)), (448, 896, 2, (0, 1, 2, 3)), (896, 1280, 3, (0, 1, 2, 3))]
+STRESS = ("aa", "av", "av", "av")
 
 
 def R(name, lo=0, hi=None, st=1):
@@ -84,7 +85,6 @@ def _two(r):
 
 def build():
     ops = []
-    boost = [0.0]
 
     def add(eng, fn, wr, rd, cost, ninc=1, after=(), sem=None):
         w, r = [], []
@@ -99,13 +99,13 @@ def build():
                     r += [t[1], t[2]]
                 else:
                     r.append(t)
-        ops.append({"eng": eng, "fn": fn, "w": w, "r": r, "cost": cost, "ninc": ninc, "after": list(after), "sem": sem, "boost": boost[0]})
+        ops.append({"eng": eng, "fn": fn, "w": w, "r": r, "cost": cost, "ninc": ninc, "after": list(after), "sem": sem})
         return len(ops) - 1
 
     def vcost(out, ins, base):
         n = _n(out)
         if out[0] == "*":
-            return 0.05 + 3.8 * n * CYC
+            return 0.05 + SCATTER * n * CYC
         if ins[0][0] == "*":
             return 0.05 + GATHER * n * CYC
         return 0.02 + max(64, base * n) * CYC
@@ -177,6 +177,10 @@ def build():
             return both(i, act1(out, a, AF.Sign))
         return i
 
+    def lin(out, a, scale, bias):
+        i = act1(out, a, AF.Identity, bias=bias, scale=scale)
+        return both(i, ts1(out, a, scale, A.mult, bias, A.add))
+
     def mm(items, first=True, last=True):
         def fn(g, T):
             res = []
@@ -194,9 +198,12 @@ def build():
         ndma[0] += 1
         return add("s", fn, wr, rd, cost, sem="dma%d" % (ndma[0] - 1))
 
-    def exchange(s, src, dst):
-        k = add("g", ("send", s), [], [src], 0.6, ninc=0)
-        add("x", ("arr", s), [dst], [], XLAT, after=[k], sem="arr%d" % s)
+    def exchange(s, parts):
+        name, at = ("mw", 0) if s == NP else ("win", s * W)
+        k = add("g", ("send", s, parts), [], [R(name, at + CUT[h], at + CUT[h + 1]) for h in parts], SEND, ninc=0)
+        for h in parts:
+            add("x", None, [R(name, at + V + G * b + CUT[h], at + V + G * b + CUT[h + 1]) for b in range(4)], [],
+                XLAT if len(parts) == 2 else XHALF[h], after=[k], sem="arr%d%s" % (s, "ab"[h]))
         return k
 
     def m16(k):
@@ -208,29 +215,34 @@ def build():
     def col(k):
         return R("col", k, k + 1)
 
-    SEL, DIAG, NI16, CF, CW, I16, I16S = 0, 16, 32, 33, 37, 39, 40
-    N64, N1024, CMI, MI, LTRI, WAD, BM4, WPA, WPD, BLK, IB, LW, NMI = 0, 1, 2, 3, 4, 5, 6, 7, 8, 9, 10, 11, 15
+    SEL, NI16, CF, CW, I16, I16S = 0, 16, 17, 21, 23, 24
+    N64, N1024, CMI, LTRI, WAD, BM4, WPA, WPD, BLK, IB, LW = range(11)
     cP, cG, cI, cR, cT, cQ4, cTQ, cFA, cFC, cFB, cFD, cAD = range(12)
 
     def win(s, lo=0, hi=W):
         return R("win", s * W + lo, s * W + hi)
 
-    def diag(out, name, lo, hi):
-        return [(out, m16(DIAG + i), R(name, lo + i, hi, 16)) for i in range(16)]
+    def row(i):
+        return R("e16", 15 - i, 143 - i)
 
-    dma(lambda q, T: q.dma_start(T.xi[:, 0:G], T.x[:, 0:G]), [R("xi", 0, G)], [])
+    def diag(out, name, lo, hi):
+        return [(out, row(i), R(name, lo + i, hi, 16)) for i in range(16)]
+
+    def centred(f, out, s, src):
+        return f(out, src, AF.Copy) if s else f(out, src, AF.Identity, bias=-2048.0)
+
+    dma(lambda q, T: q.dma_start(T.win[:, 0:G], T.x[:, 0:G]), [win(0, 0, G)], [])
     dma(lambda q, T: q.dma_start(T.nbi[:], T.nb[:]), [R("nbi")], [])
-    dma(lambda q, T: q.dma_start(T.xi[:, G:V], T.x[:, G:V]), [R("xi", G, V)], [], 2.8)
+    dma(lambda q, T: q.dma_start(T.win[:, G:V], T.x[:, G:V]), [win(0, G, V)], [], 2.8)
     for k, nm in enumerate(("lb", "pk", "pl", "hq", "pj")):
         dma(lambda q, T, k=k, nm=nm: q.dma_start(T.l32[:, 8 * k:8 * k + 8], T[nm][:]), [R("l32", 8 * k, 8 * k + 8)], [])
     dma(lambda q, T: q.dma_start(T.mw[:, 0:V], T.am[:]), [R("mw", 0, V)], [], 2.6)
-    add("g", lambda g, T: [g.iota(T.ji[:], [[1, 128]], 0, 0)], [R("ji")], [], 0.4)
-    add("g", lambda g, T: [g.iota(T.pi[:, 0:1], [[0, 1]], 0, 1)], [R("pi", 0, 1)], [], 0.15)
-    ts(win(0, 0, G), R("xi", 0, G), -2048.0, A.add)
-    k0 = exchange(0, win(0, 0, G), win(0, V, W))
-    add("g", lambda g, T: [g.iota(T.tab[:], [[1, 1296]], 0, 0)], [R("tab")], [], 2.7, after=[k0])
-    exchange(NP, R("mw", 0, G), R("mw", V, W))
-    ts(win(0, G, V), R("xi", G, V), -2048.0, A.add)
+    dma(lambda q, T: q.dma_start(T.xi[:], T.x[:]), [R("xi")], [], 4.0)
+    add("g", lambda g, T: [g.iota(T.pi[:, 0:1], [[0, 1]], 0, 1)], [R("pi", 0, 1)], [], 0.27)
+    add("g", lambda g, T: [g.iota(T.ji[:], [[1, 144]], 0, 0)], [R("ji")], [], 0.45)
+    k0 = exchange(0, (0, 1))
+    add("g", lambda g, T: [g.iota(T.tab[:], [[1, V]], 0, 0)], [R("tab")], [], 2.7, after=[k0])
+    exchange(NP, (0, 1))
     cp(R("off", 0, 320), R("nbi"))
     ts(R("nb16"), R("nbi"), -C0, A.add)
 
@@ -242,8 +254,8 @@ def build():
     ts(R("pi", 5, 6), p0, 2, A.arith_shift_right)
     cp(R("col", 0, 6), R("pi", 0, 6))
     cp(R("jf"), R("ji"))
-    ts(R("i32m"), R("jf"), col(cP), A.is_equal)
-    ts(R("ti"), R("ji"), 4, A.arith_shift_right)
+    ts(R("i32m"), R("jf", 0, 128), col(cP), A.is_equal)
+    ts(R("ti"), R("ji", 0, 128), 4, A.arith_shift_right)
     ts(R("jt", 0, 128), R("ti"), col(cG), A.is_equal)
     blk, eye = R("jt", 0, 128), R("i32m")
     ts(R("mq"), R("jf", 0, 16), col(cI), A.is_equal)
@@ -264,14 +276,16 @@ def build():
             cp(R("nbw", 320 * q, 320 * q + 320), b)
         else:
             act(R("nbw", 320 * q, 320 * q + 320), b, AF.Copy)
-    for q in range(16):
-        ts(m16(DIAG + q), m16(I16), R("mq", q, q + 1), A.mult)
+    ts(col(16), col(cP), 15.0, A.add)
+    ts(R("e16"), R("jf"), col(16), A.is_equal, R("mq", 0, 1), A.mult)
+    ts(col(17), col(cG), 16.0, A.mult, 15.0, A.add)
+    ts(R("fb16"), R("jf"), col(17), A.is_equal)
     ms(R("ones"), 1.0)
     act(m16(I16S), eye, AF.Copy, scale=0.0625)
-    for k, c in ((N64, -64.0), (N1024, -1024.0), (CMI, -15.0 / 32), (MI, M), (NMI, -M), (IB, 1.0)):
+    for k, c in ((N64, -64.0), (N1024, -1024.0), (CMI, -15.0 / 32), (IB, 1.0)):
         act(mb(k), eye, AF.Copy, scale=c)
     for lo, hi in CH:
-        act(R("x16", lo, hi), win(0, lo, hi), AF.Copy)
+        centred(act, R("x16", lo, hi), 0, win(0, lo, hi))
     act(m16(NI16), eye, AF.Copy, scale=-1.0)
     red(col(cFA), R("mq", 4, 7))
     red(col(12), R("mq", 7, 9))
@@ -286,9 +300,9 @@ def build():
         act(m16(CF + r), eye, AF.Copy, scale=col(c))
     ts(m16(CW), m16(I16), R("mr", 0, 1), A.mult, -1.0, A.mult)
     ts(m16(CW + 1), m16(I16), R("mr", 3, 4), A.mult, -1.0, A.mult)
-    ts(R("ti"), R("ji"), 2, A.arith_shift_right)
+    ts(R("ti"), R("ji", 0, 128), 2, A.arith_shift_right)
     ts(R("tb"), R("ti"), col(cQ4), A.is_equal)
-    ts(R("tw"), R("jf"), col(cP), A.is_gt)
+    ts(R("tw"), R("jf", 0, 128), col(cP), A.is_gt)
     tt(mb(LTRI), R("tb"), R("tw"), A.mult)
     act(mb(WAD), blk, AF.Copy, scale=col(cAD))
     act(mb(BM4), blk, AF.Copy, scale=-4.0)
@@ -305,7 +319,6 @@ def build():
     cp(R("lu"), R("l32"))
     cp(R("lf"), R("l32"))
     cp(R("rep", 0, 128), IND(R("tab"), R("lu", 0, 8)))
-    cp(R("rep", 128, 256), IND(R("tab", 0, 32), R("lu", 24, 32)))
     ts(R("lq16"), R("lf", 16, 24), 0.25, A.mult)
     ts(R("ti", 0, 8), R("l32", 0, 8), 4, A.arith_shift_right)
     ts(R("tw", 0, 8), R("ti", 0, 8), -5119.0, A.mult)
@@ -329,7 +342,7 @@ def build():
 
     def place(v, n, at):
         ts(R("ti", at, at + n), v, 0.0625, A.mult, HI0, A.add)
-        ts(R("tb", at, at + n), v, 320.0, A.mult, B0, A.add)
+        ts(R("tb", at, at + n), v, 320.0, A.mult, B0, A.add) if n == 4 else lin(R("tb", at, at + n), v, 320.0, B0)
 
     def place_sum(out, n, at):
         ts(R("tw", at, at + n), R("ti", at, at + n), -5119.0, A.mult)
@@ -339,23 +352,22 @@ def build():
 
     def names(h):
         act1(R("nm16", 0, 512), IND(nbw, R("o2", 0, 32)), AF.Copy)
-        if h:
+        if h or NM0 == "a":
             act(R("nm16", 512, 1024), IND(nbw, R("o2", 32, 64)), AF.Copy)
         else:
             cp1(R("nm16", 512, 1024), IND(nbw, R("o2", 32, 64)))
 
     def names_list(h):
         mm(diag(R("L1", 256, 320), "nm16", 0, 1024))
-        ts(R("o4", 64 * h, 64 * h + 64), R("L1", 256, 320), C0, A.add)
+        lin(R("o4", 64 * h, 64 * h + 64), R("L1", 256, 320), 1.0, C0)
 
     def switch(flag, h, t, dst):
-        mm(diag(R("L2", 480, 484), "wn16", flag, flag + 64))
         for c in range(4):
-            ts(R("osc", 16 * h + c, 16 * h + 16, 4), R("dn", c, 16, 4), R("L2", 480 + c, 481 + c), A.mult, R("spare", c, c + 1), A.add)
+            ts(R("osc", 16 * h + c, 16 * h + 16, 4), R("dn", c, 16, 4), R(flag[0], flag[1] + c, flag[1] + c + 1), A.mult, R("spare", c, c + 1), A.add)
         for k, u in enumerate((2, 3, 0, 1) if h else (1, 0, 3, 2)):
             cp(IND(nbw, R("osc", 16 * h + 4 * u, 16 * h + 4 * u + 4)), R("at16", 256 * t + 64 * k, 256 * t + 64 * k + 64))
         dma(lambda q, T: q.dma_start(T.off32[:], T.nbw[0:128:18, 0:5120]), [R("off32")], [R("nbw", 0, 5120)], 2.8)
-        ts(R("off", 320 * dst, 320 * dst + 320), R("off32"), C0, A.add)
+        lin(R("off", 320 * dst, 320 * dst + 320), R("off32"), 1.0, C0)
 
     def lanes(t, dst):
         a0 = 256 * t
@@ -377,14 +389,14 @@ def build():
         for p in range(4):
             ts(R("o2", 16 * p, 16 * p + 16), R("to", 0, 16), 80.0 * p, A.add)
         ts(R("eg"), R("at16", a0, a0 + 256), -128.0, A.is_ge)
-        ts(R("o3"), R("al"), C0, A.add)
+        ts(R("o3"), R("al"), C0, A.add, V - 1.0, A.min)
         names(0)
         tt(R("dn"), R("to", 0, 16), R("pt", 16 * t, 16 * t + 16), A.subtract)
         uf, uw, n2 = R("L0", 0, 64), R("L0", 64, 128), R("L2", 128, 192)
         ad = [(i, R("nm16", 64 * (4 * (i % 4) + i // 4), 64 * (4 * (i % 4) + i // 4 + 1))) for i in (0, 1, 2, 3, 12, 13, 14, 15)]
         mm([(uf, m16(CF + r), at(r)) for r in range(4)] + [(uw, m16(CW), at(2)), (uw, m16(CW + 1), at(1))])
         act(R("tm"), R("L0", 0, 128), AF.Copy, scale=-1.0)
-        mm([(n2, m16(DIAG + i), u) for i, u in ad])
+        mm([(n2, row(i), u) for i, u in ad])
         tt(R("eb", 64, 128), n2, R("tm", 64, 128), A.is_equal)
         tt(R("eb", 0, 64), n2, R("tm", 0, 64), A.is_equal)
         mm([(R("L2", 256, 320), mb(LTRI), R("eb", 64, 128))])
@@ -393,7 +405,7 @@ def build():
         sc = R("L2", 0, 64)
         mm([(sc, mb(N64), R("eg", 64 * r, 64 * r + 64)) for r in (0, 1, 3)] + [(sc, mb(BM4), R("eb", 0, 64)), (sc, mb(WAD), chg),
             (R("L2", 64, 128), mb(WPA), chg), (R("L2", 128, 192), mb(WPD), chg)])
-        ts(R("gp16"), R("L2", 0, 192), -1.0, A.add, 0.0, A.max)
+        both(act1(R("gp16"), R("L2", 0, 192), AF.Relu, bias=-1.0), ts1(R("gp16"), R("L2", 0, 192), -1.0, A.add, 0.0, A.max))
         for r in range(4):
             for c in range(4):
                 k = 4 * c + r
@@ -410,24 +422,28 @@ def build():
         mm([(R("L2", 384, 448), mb(LW + c), R("sb", 64 * c, 64 * c + 64)) for c in range(4)])
         tt(R("thg"), R("thr"), R("gp16", 0, 64), A.mult)
         tt(R("wn16", 0, 64), R("L2", 384, 448), R("thg"), A.is_lt)
-        switch(0, 0, t, dst)
-        ts(R("hqw", 0, 64), R("wn16", 0, 64), -99.0, A.mult, 99.0, A.add)
-        tt(R("hqw", 64, 128), R("hqw", 0, 64), R("rep", 128 + 64 * t, 192 + 64 * t), A.add)
+        mm(diag(R("L2", 480, 484), "wn16", 0, 64))
+        switch(R("L2", 480, 484), 0, t, dst)
+        lin(R("hqw", 0, 4), R("L2", 480, 484), -99.0, 99.0)
+        tt(R("hqw", 4, 8), R("hqw", 0, 4), R("lf", 24 + 4 * t, 28 + 4 * t), A.add)
 
     def stress(s, h):
-        act(R("xo"), IND(win(s), R("o3")), AF.Copy)
+        centred(act, R("xo"), s, IND(win(s, 0, V), R("o3")))
         for u in range(2):
             a, b = 512 * u, 512 * u + 512
-            act(R("ld", a, b), IND(win(s), R("o4", 64 * h + 32 * u, 64 * h + 32 * u + 32)), AF.Copy)
             bk = "L%d" % u
-            for v in range(2):
-                o = R(bk, 256 * v, 256 * v + 256)
-                mm([(o, m16(I16), R("ld", a + 256 * v, a + 256 * v + 256)), (o, m16(NI16), R("xo"))])
-            ts(R("lc", a, b), R(bk), -2047.0, A.max, 2047.0, A.min)
-            if h and u < LSV:
-                ts(R("ls", a, b), R("lc", a, b), -1.0, A.max, 1.0, A.min)
+            if STRESS[s // 3 * 2 + h][u] == "a":
+                centred(act, R("ld", a, b), s, IND(win(s), R("o4", 64 * h + 32 * u, 64 * h + 32 * u + 32)))
+                for v in range(2):
+                    o = R(bk, 256 * v, 256 * v + 256)
+                    mm([(o, m16(I16), R("ld", a + 256 * v, a + 256 * v + 256)), (o, m16(NI16), R("xo"))])
+                ts(R("lc", a, b), R(bk), -2047.0, A.max, 2047.0, A.min)
             else:
-                act(R("ls", a, b), R("lc", a, b), AF.Sign)
+                for v in range(2):
+                    at = 64 * h + 32 * u + 16 * v
+                    tt(R("ld", a + 256 * v, a + 256 * v + 256), IND(win(s), R("o4", at, at + 16)), R("xo"), A.subtract)
+                ts(R("lc", a, b), R("ld", a, b), -2047.0, A.max, 2047.0, A.min)
+            ts(R("ls", a, b), R("lc", a, b), -1.0, A.max, 1.0, A.min)
             mm([(R(bk), m16(I16), R("lc", a, b)), (R(bk), mb(N1024), R("ls", a, b))])
             act(R("sq", a, b), R(bk), AF.Square)
         for u in range(2):
@@ -437,14 +453,14 @@ def build():
 
     def votes(t, dst):
         tt(R("wb"), R("L0", 0, 64), R("sf"), A.is_gt)
-        mm([(R("L2", 384, 448), mb(BLK), R("wb"))])
-        tt(R("wn16", 64, 128), R("L2", 384, 448), R("hqw", 64, 128), A.is_ge)
-        switch(64, 1, t, dst)
+        mm([(R("L2", 384, 388), R("fb16", 15 - i, 143 - i), R("wb", i, 64, 16)) for i in range(16)])
+        tt(R("hqw", 8, 12), R("L2", 384, 388), R("hqw", 4, 8), A.is_ge)
+        switch(R("hqw", 8, 12), 1, t, dst)
 
     turn = [0, 0]
 
-    def diffs(s, k, o, nact):
-        lo, hi, bank = k
+    def diffs(s, k, o):
+        lo, hi, nact, onv = k
         m = hi - lo
         b = turn[0] % NSET
         turn[0] += 1
@@ -457,55 +473,53 @@ def build():
         for p in range(4 - nact, 4):
             xk = R("X%d" % (turn[1] % 3), 0, m)
             turn[1] += 1
-            act1(sl("d16", p), offs(p), AF.Copy)
+            centred(act1, sl("d16", p), s, offs(p))
             mm([(xk, m16(NI16), R("x16", V * s + lo, V * s + hi)), (xk, m16(I16), sl("d16", p))])
             ts(sl("c16", p), xk, -2047.0, A.max, 2047.0, A.min)
         for p in range(4 - nact):
-            tt(sl("d16", p), offs(p), R("x16", V * s + lo, V * s + hi), A.subtract)
+            tt(sl("d16", p), offs(p), R("x16", V * s + lo, V * s + hi) if s else R("xi", lo, hi), A.subtract)
         one = s == NP - 1
-        for p, n in [(p, 1) for p in range(4 - nact)] if one else ((0, 4 - nact),):
+        mine = [(p, 1) for p in range(4 - nact)] if one or nact == 4 else [(0, 4 - nact)]
+        for p, n in mine:
             ts(sl("c16", p, n), sl("d16", p, n), -2047.0, A.max, 2047.0, A.min)
-        for p, n in ((0, 1), (1, 1), (2, 1), (3, 1)) if one else (((0, 2), (2, 1), (3, 1)) if lo == 0 else ((0, 2), (2, 2))):
+        for p, n in mine + ([(p, 1) for p in range(4 - nact, 4)] if one or lo < G else [(4 - nact, nact)]):
             src = sl("d16" if p + n <= 4 - nact else "c16", p, n)
-            if p == 2 and bank in (SIGNF if one else SIGNV):
+            if p in onv:
                 ts(sl("s16", p, n), src, -1.0, A.max, 1.0, A.min)
             else:
                 act(sl("s16", p, n), src, AF.Sign)
-        return b, sl
+        return sl
 
     def sweep(s, o):
         xa, xb = V * s, V * (s + 1)
-        for k in SUB:
-            lo, hi, bank = k
-            boost[0] = -LATER * lo / V
+        for k in (SUB0, SUB1, SUB2)[s % 3]:
+            lo, hi = k[:2]
             m = hi - lo
             tb = R("T%d" % (turn[0] % 2), 0, m)
             mm([(tb, m16(I16), R("x16", xa + lo, xa + hi)), (tb, mb(CMI), R("ones", 0, m))], last=False)
-            b, sl = diffs(s, k, o, 3 if lo in MORE else 2)
-            for kind, p in ("c0", "c1", "s0", "s1", "c2", "s2", "c3", "s3") if lo == 0 else ("c0", "c1", "s0", "s1", "c2", "c3", "s2", "s3"):
-                end = kind + p == "s3"
-                mm([(tb, m16(I16S) if kind == "c" else mb(N64), sl(kind + "16", int(p)))] + ([(tb, mb(MI), R("ones", 0, m)), (tb, mb(NMI), R("ones", 0, m))] if end else []),
-                   first=False, last=end)
+            sl = diffs(s, k, o)
+            for kind, p in ("c0", "c1", "s0", "s1", "c2", "s2", "c3", "s3") if lo < G else ("c0", "c1", "s0", "s1", "c2", "c3", "s2", "s3"):
+                mm([(tb, m16(I16S) if kind == "c" else mb(N64), sl(kind + "16", int(p)))], first=False, last=kind + p == "s3")
             ts(win(s + 1, lo, hi), tb, -2048.0, A.max, 2047.0, A.min)
-            if lo == 0:
-                exchange(s + 1, win(s + 1, 0, G), win(s + 1, V, W))
-            if hi == CH[bank][1]:
-                lo = CH[bank][0]
-                act(R("x16", xb + lo, xb + hi), win(s + 1, lo, hi), AF.Copy)
-        boost[0] = 0.0
+            sent = [exchange(s + 1, (CUT.index(lo),))] if hi <= G else []
+            if hi < G:
+                continue
+            if hi == G:
+                lo, m = 0, G
+            add("g", lambda g, T, lo=lo, hi=hi: [g.affine_select(T.x16[:, xb + lo:xb + hi], _ap(T, win(s + 1, lo, hi)), [[0, hi - lo]], A.is_equal, 0.0, 0, 0)],
+                [R("x16", xb + lo, xb + hi)], [win(s + 1, lo, hi)], 0.2 + 2 * m * CYC, after=sent)
 
     def final(s, o):
         nf = 0
         for k in FSUB:
-            lo, hi, bank = k
-            boost[0] = -LATEF * lo / V
+            lo, hi = k[:2]
             m = hi - lo
             yb = R("T%d" % (turn[0] % 2), 0, m)
-            b, sl = diffs(s, k, o, 2 if lo in MOREF else 1)
+            sl = diffs(s, k, o)
             for p in (3, 0, 1, 2):
                 fb = R("L%d" % (nf % 3), 0, m)
-                e = win(0, CM * (nf % 4), CM * (nf % 4) + m)
-                tq = win(1, CM * (nf % 4), CM * (nf % 4) + m)
+                e = R("fe", CM * (nf % 4), CM * (nf % 4) + m)
+                tq = R("fq", CM * (nf % 4), CM * (nf % 4) + m)
                 nf += 1
                 mm([(fb, m16(I16), sl("c16", p)), (fb, mb(N1024), sl("s16", p))])
                 act(e, fb, AF.Square)
@@ -513,8 +527,8 @@ def build():
                 tt(tq, IND(R("mw"), R("off", 320 * o + 80 * p + lo // 16, 320 * o + 80 * p + hi // 16)), e, A.mult)
                 if p != 2:
                     mm([(yb, R("i32m"), tq)], first=p == 3, last=p == 1)
-            tt(win(2, lo, hi), yb, tq, A.add)
-            dma(lambda q, T, lo=lo, hi=hi: q.dma_start(T.y[:, lo:hi], T.win[:, 2 * W + lo:2 * W + hi]), [], [win(2, lo, hi)])
+            tt(R("fy", lo, hi), yb, tq, A.add)
+            dma(lambda q, T, lo=lo, hi=hi: q.dma_start(T.y[:, lo:hi], T.fy[:, lo:hi]), [], [R("fy", lo, hi)])
 
     for t in range(2):
         lanes(t, 2 * t + 1)
@@ -553,70 +567,80 @@ def schedule(ops):
         o["deps"] = sorted(deps)
     n = len(ops)
 
-    def lat(j, i):
-        a, b = ops[j]["eng"], ops[i]["eng"]
-        return 0.0 if a == b == "t" or b == "x" else (SAME if a == b else CROSS)
+    pred = [o["deps"] for o in ops]
     succ = [[] for _ in range(n)]
-    for i, o in enumerate(ops):
-        for j in o["deps"]:
+    for i in range(n):
+        for j in pred[i]:
             succ[j].append(i)
-    prio = [0.0] * n
-    for i in range(n - 1, -1, -1):
-        prio[i] = ops[i]["cost"] + max([prio[k] + lat(i, k) + HOP for k in succ[i]] + [0.0])
-    prio = [p + o["boost"] + NOISE * math.sin(SEED * (i + 1.0) ** 1.1) for i, (p, o) in enumerate(zip(prio, ops))]
-    left = [len(o["deps"]) for o in ops]
-    ready = {i: 0.0 for i in range(n) if not left[i]}
-    free = {e: 0.0 for e in "vatgsx"}
-    order = {e: [] for e in "vatgsx"}
-    end = [0.0] * n
-    seq = []
-    while ready:
-        best = min(max(t, free[ops[i]["eng"]]) for i, t in ready.items())
-        take = [i for i, t in ready.items() if "alt" in ops[i] and max(t, free[ops[i]["alt"][0]]) < best
-                and max(t, free[ops[i]["alt"][0]]) + ops[i]["alt"][2] < max(t, free[ops[i]["eng"]]) + ops[i]["cost"] + STEAL[ops[i]["alt"][0]]
-                and not any(ops[c]["eng"] == ops[i]["alt"][0] and u < max(t, free[ops[c]["eng"]]) + IDLE for c, u in ready.items())]
-        if take:
-            o = ops[max(take, key=lambda c: (prio[c], -c))]
-            o["eng"], o["fn"], o["cost"] = o.pop("alt")
-            continue
-        cand = [i for i, t in ready.items() if max(t, free[ops[i]["eng"]]) <= best + 0.04]
-        e = ops[min(cand, key=lambda i: (max(ready[i], free[ops[i]["eng"]]), i))]["eng"]
-        i = max([c for c in cand if ops[c]["eng"] == e], key=lambda c: (prio[c], -c))
-        soon = [c for c, t in ready.items() if ops[c]["eng"] == e and t <= best + min(LOOK, ops[i]["cost"]) and prio[c] > prio[i] + GAP]
-        if soon:
-            i = max(soon, key=lambda c: (prio[c], -c))
-        st = max(ready.pop(i), free[e])
-        end[i] = st + ops[i]["cost"]
-        ops[i]["start"] = st
-        free[e] = st + 0.06 if e == "s" else (0.0 if e == "x" else end[i])
-        order[e].append(i)
-        seq.append(i)
-        for k in succ[i]:
-            left[k] -= 1
-            if not left[k]:
-                ready[k] = max(end[j] + lat(j, k) for j in ops[k]["deps"])
+    forms = [[(o["eng"], o["cost"])] + ([(o["alt"][0], o["alt"][2])] if "alt" in o else []) for o in ops]
+    two = [i for i in range(n) if len(forms[i]) > 1]
 
-    def pack(keys, before, back):
-        slots = {e: [] for e in "vatg"}
-        fin = [0.0] * n
-        for i in sorted(range(n), key=lambda i: keys[i]):
-            e, c = ops[i]["eng"], ops[i]["cost"]
-            st = max([fin[j] + (lat(i, j) if back else lat(j, i)) for j in before[i]] + [0.0])
-            if e in slots:
-                sl = slots[e]
-                at = len(sl)
-                while at and sl[at - 1][1] > st:
-                    at -= 1
-                while at < len(sl) and st + c > sl[at][0] + 1e-9:
-                    st = max(st, sl[at][1])
-                    at += 1
-                sl.insert(at, (st, st + c))
-            fin[i] = st + c
+    def lat(a, b):
+        return 0.0 if a == b == "t" or b == "x" else (SAME if a == b else CROSS)
+
+    def pack(keys, before, form, back):
+        starts, ends = {e: [] for e in "vatg"}, {e: [] for e in "vatg"}
+        fin = [None] * n
+        for i0 in sorted(range(n), key=lambda i: -keys[i]):
+            todo = [i0]
+            while todo:
+                i = todo[-1]
+                if fin[i] is not None:
+                    todo.pop()
+                    continue
+                late = [j for j in before[i] if fin[j] is None]
+                if late:
+                    todo += late
+                    continue
+                e, c = forms[i][form[i]]
+                st = 0.0
+                for j in before[i]:
+                    ej = forms[j][form[j]][0]
+                    u = fin[j] + (lat(e, ej) if back else lat(ej, e))
+                    if u > st:
+                        st = u
+                if e in starts:
+                    ss, es = starts[e], ends[e]
+                    at, top = 0, len(es)
+                    while at < top:
+                        mid = (at + top) // 2
+                        if es[mid] > st:
+                            top = mid
+                        else:
+                            at = mid + 1
+                    while at < len(ss) and st + c > ss[at] + 1e-9:
+                        if es[at] > st:
+                            st = es[at]
+                        at += 1
+                    ss.insert(at, st)
+                    es.insert(at, st + c)
+                fin[i] = st + c
         return fin
-    for _ in range(PASSES):
-        fin = pack([(-round(end[i], 6), -i) for i in range(n)], succ, True)
-        end = pack([(-round(fin[i], 6), i) for i in range(n)], [o["deps"] for o in ops], False)
+    keys = [0.0] * n
+    for i in range(n - 1, -1, -1):
+        keys[i] = forms[i][0][1] + max([keys[k] + lat(forms[i][0][0], forms[k][0][0]) for k in succ[i]] + [0.0])
+    state = [SEED]
+
+    def draw():
+        state[0] = (state[0] * 1103515245 + 12345) % 2147483648
+        return state[0] / 2147483648.0
+    best, now, kept = None, None, [0] * n
+    for it in range(ROUNDS):
+        form = list(kept)
+        for _ in range(1 + int(draw() * FLIPS) if it else 0):
+            i = two[int(draw() * len(two))]
+            form[i] = 1 - form[i]
+        a = draw() * NOISE
+        fin = pack(pack([k + a * draw() for k in keys], pred, form, False), succ, form, True)
+        end = pack(fin, pred, form, False)
+        if now is None or max(end) < now + TEMP * (1 - it / ROUNDS) * draw():
+            now, kept, keys = max(end), form, fin
+        if best is None or max(end) < best[0]:
+            best = (max(end), end, form)
+    _, end, form = best
     for i, o in enumerate(ops):
+        if form[i]:
+            o["eng"], o["fn"], o["cost"] = o["alt"]
         o["start"] = end[i] - o["cost"]
     seq = sorted(range(n), key=lambda i: (round(ops[i]["start"], 6), i))
     order = {e: [i for i in seq if ops[i]["eng"] == e] for e in "vatgsx"}
@@ -627,8 +651,8 @@ def schedule(ops):
         o = ops[i]
         e = o["eng"]
         if e == "x":
-            o["tag"] = (o["sem"], 32)
-            clock[i] = {o["sem"]: 32}
+            o["tag"] = (o["sem"], 16)
+            clock[i] = {o["sem"]: 16}
             continue
         kn = known[e]
         waits = []
@@ -667,7 +691,7 @@ def helpers(core, T, topo):
     r = T.rank_of(core)
     dsts = [T.cores[(r + d) % len(T.cores)] for d in DS]
     hs = [c for c in topo.cores_of(core) if c != core and all(topo.may_write(c, d) for d in dsts)]
-    hs.sort(key=lambda c: (topo.die(c) != topo.die(core), c))
+    hs.sort(key=lambda c: (topo.die(c) == topo.die(core), c))
     return hs[:4], dsts
 
 
@@ -684,14 +708,14 @@ def helper_program(g, core, owner, T, topo):
     k = hs.index(core)
     total = 0
     for s in [0, NP] + list(range(1, NP)):
-        g.wait_ge(T.sem["rel%d" % s], 8)
+        g.wait_ge(T.sem["rel%d" % s], 8 if s in (0, NP) else 16)
         trs = []
         for u in range(2):
             b = 2 * (k % 2) + u
             rid, pid = topo.addr(dsts[b], core)
             engs = topo.engines(core, dsts[b])
             trs.append(RemoteDMATransfer(dst_ids=[DstId(rid=rid, pnc=pid)], dma_engine_mask=_mask(engs[4 * u:4 * u + 4]),
-                                         remote_sem=T.sem["arr%d" % s], src=_slot(T, s, 16 * b),
+                                         remote_sem=T.sem["arr%d%s" % (s, "ab"[k // 2])], src=_slot(T, s, 16 * b),
                                          dst=_cols(T, s, V + G * b + H * (k // 2))))
         g.remote_dma_fused(trs, local_sem=T.sem.sent)
         total += 8
@@ -716,12 +740,17 @@ def rank_program(g, core, T, topo):
             if e == "s":
                 o["fn"](q, T).then_inc(T.sem[o["sem"]], 16)
             elif isinstance(o["fn"], tuple):
-                s = o["fn"][1]
+                _, s, parts = o["fn"]
                 trs = []
                 for k, h in enumerate(hs):
+                    if k // 2 not in parts:
+                        continue
                     rid, pid = topo.addr(h, core)
                     engs = topo.engines(core, h)
-                    trs.append(RemoteDMATransfer(dst_ids=[DstId(rid=rid, pnc=pid)] * 2, dma_engine_mask=_mask(engs[4 * k:4 * k + 4]),
+                    if len(parts) == 2:
+                        engs = engs[k // 2::2]
+                    n = len(engs) // 2
+                    trs.append(RemoteDMATransfer(dst_ids=[DstId(rid=rid, pnc=pid)] * 2, dma_engine_mask=_mask(engs[n * (k % 2):n * (k % 2) + n]),
                                                  remote_sem=T.sem["rel%d" % s], srcs=[_cols(T, s, H * (k // 2))],
                                                  dsts=[_slot(T, s, 0), _slot(T, s, 128)]))
                 g.remote_dma_fused(trs, local_sem=T.sem.sent)

import math
from concourse.bass import DstId, RemoteDMATransfer
from concourse.mybir import AluOpType, AxisListType, ActivationFunctionType

V, G, W = 1280, 384, 2816
DS = [1, 2, 6, 7]
H = G // 2
CUT = [0, H, G]
C0 = 1408.0
CH = [(0, 384), (384, 832), (832, 1280)]
CM, NSET = 448, 2
NP = 7
F32, F16, B16, I32, U16 = "float32", "float16", "bfloat16", "int32", "uint16"


def _sb(n, dt):
    return ("sbuf", [128, n], dt)


SCRATCH = {
    "win": _sb(NP * W, I32), "mw": _sb(W, B16), "nbw": _sb(5376, F32), "x16": _sb(NP * V, F16), "xi": _sb(V, I32),
    "fe": _sb(4 * CM, F32), "fq": _sb(4 * CM, F32), "fy": _sb(V, F32), "e16": _sb(144, F16),
    "nbi": _sb(320, I32), "nb16": _sb(320, F16), "off": _sb(5 * 320, U16), "off32": _sb(320, F32),
    "d16": _sb(4 * NSET * CM, F16), "c16": _sb(4 * NSET * CM, F16), "s16": _sb(4 * NSET * CM, B16),
    "m16": _sb(25 * 128, F16), "mb": _sb(14 * 128, B16), "i32m": _sb(128, F32), "ones": _sb(CM, B16),
    "ji": _sb(144, I32), "jf": _sb(144, F32), "jt": _sb(256, F32), "pi": _sb(8, I32), "col": _sb(32, F32),
    "mq": _sb(16, F32), "mr": _sb(4, F32), "tab": _sb(V, I32), "fb16": _sb(144, B16),
    "l32": _sb(40, I32), "lu": _sb(40, U16), "lf": _sb(40, F32), "rep": _sb(256, F32),
    "lq16": _sb(8, F16), "w4": _sb(4, F32), "thr": _sb(64, F32), "spare": _sb(16, F32),
    "ti": _sb(128, I32), "tb": _sb(128, F32), "tw": _sb(128, F32), "to": _sb(128, F32),
    "o1": _sb(16, U16), "o1f": _sb(16, F32), "oc": _sb(4, U16), "o2": _sb(64, U16), "o3": _sb(16, U16), "o4": _sb(128, U16),
    "osc": _sb(32, U16), "at16": _sb(512, F16), "nm16": _sb(1024, F16), "eb": _sb(256, B16), "eg": _sb(256, B16),
    "gp16": _sb(192, F16), "eq": _sb(4096, B16), "sb": _sb(256, B16), "al": _sb(16, F32), "pt": _sb(32, F32),
    "vt": _sb(16, F32), "dn": _sb(16, F32), "tm": _sb(128, F32), "thg": _sb(64, F32),
    "wn16": _sb(64, F16), "hqw": _sb(16, F32), "wb": _sb(64, B16),
    "xo": _sb(256, F16), "sq": _sb(1024, F32), "sf": _sb(64, F32),
    "ld": _sb(1024, F16), "lc": _sb(1024, F16), "ls": _sb(1024, B16),
    "hop": ("dram", [NP * 256, H], I32), "hopm": ("dram", [256, H], B16),
}
for _n in ("X0", "X1", "X2", "T0", "T1", "L0", "L1", "L2"):
    SCRATCH[_n] = ("psum", [128, 512], F32)
NDMA = 20
SEMAPHORES = (["qv", "qa", "qt", "qg", "sent"] + ["arr%d%s" % (s, h) for s in range(NP + 1) for h in "ab"] + ["rel%d" % s for s in range(NP + 1)]
              + ["dma%d" % k for k in range(NDMA)])
A = AluOpType
AF = ActivationFunctionType
CYC, PEC = 1.0e-3, 0.5e-3
XLAT, GATHER, SCATTER, SEND = 10.0, 1.56, 3.8, 0.6
SAME, CROSS = 0.15, 0.3
SUB0 = SUB1 = SUB2 = [(0, H, 2, (3,)), (H, G, 2, (3,)), (G, 832, 2, ()), (832, 1152, 2, ()), (1152, V, 2, ())]
XHALF = (10.0, 8.5)
ROUNDS, NOISE, FLIPS, TEMP, SEED = 1500, 0.3, 3, 0.3, 1
NM0 = "a"
FSUB = [(0, 448, 3, (0, 1, 2, 3)), (448, 896, 2, (0, 1, 2, 3)), (896, 1280, 3, (0, 1, 2, 3))]
STRESS = ("aa", "av", "av", "av")


def R(name, lo=0, hi=None, st=1):
    return (name, lo, SCRATCH[name][1][1] if hi is None else hi, st)


def IND(w, o):
    return ("*", w, o)


def _n(r):
    return 16 * _n(r[2]) if r[0] == "*" else (r[2] - r[1] + r[3] - 1) // r[3]


def _ap(T, r):
    if not isinstance(r, tuple):
        return r
    if r[0] == "*":
        return _ap(T, r[1]).indirect(_ap(T, r[2]))
    return T[r[0]][:, r[1]:r[2]] if r[3] == 1 else T[r[0]][:, r[1]:r[2]:r[3]]


def _ps(r):
    return r[0] != "*" and SCRATCH[r[0]][0] == "psum"


def _two(r):
    return r[0] != "*" and SCRATCH[r[0]][2] in (F16, B16, U16)


def build():
    ops = []

    def add(eng, fn, wr, rd, cost, ninc=1, after=(), sem=None):
        w, r = [], []
        for t in wr:
            if t[0] == "*":
                w.append(t[1]); r.append(t[2])
            else:
                w.append(t)
        for t in rd:
            if isinstance(t, tuple):
                if t[0] == "*":
                    r += [t[1], t[2]]
                else:
                    r.append(t)
        ops.append({"eng": eng, "fn": fn, "w": w, "r": r, "cost": cost, "ninc": ninc, "after": list(after), "sem": sem})
        return len(ops) - 1

    def vcost(out, ins, base):
        n = _n(out)
        if out[0] == "*":
            return 0.05 + SCATTER * n * CYC
        if ins[0][0] == "*":
            return 0.05 + GATHER * n * CYC
        return 0.02 + max(64, base * n) * CYC

    def ts(out, a, s1, o0, s2=None, o1=None):
        def fn(g, T):
            if o1 is None:
                return [g.vector.tensor_scalar(_ap(T, out), _ap(T, a), _ap(T, s1), None, o0)]
            return [g.vector.tensor_scalar(_ap(T, out), _ap(T, a), _ap(T, s1), _ap(T, s2), o0, o1)]
        return add("v", fn, [out], [a, s1, s2], vcost(out, [a], 0.5 if _two(out) and _two(a) else 1))

    def tt(out, a, b, o):
        return add("v", lambda g, T: [g.vector.tensor_tensor(_ap(T, out), _ap(T, a), _ap(T, b), o)], [out], [a, b],
                   vcost(out, [a], 1 if _ps(a) or _ps(b) else 2))

    def cp(out, a):
        return add("v", lambda g, T: [g.vector.tensor_copy(_ap(T, out), _ap(T, a))], [out], [a],
                   vcost(out, [a], 0.5 if _two(out) and _two(a) else 1))

    def ms(out, c):
        return add("v", lambda g, T: [g.vector.memset(_ap(T, out), c)], [out], [], vcost(out, [out], 1))

    def red(out, a):
        return add("v", lambda g, T: [g.vector.tensor_reduce(_ap(T, out), _ap(T, a), AxisListType.X, A.add)], [out], [a], 0.09)

    def scan(out, a, b):
        return add("v", lambda g, T: [g.vector.tensor_tensor_scan(_ap(T, out), _ap(T, a), _ap(T, b), 0.0, A.mult, A.add)],
                   [out], [a, b], vcost(out, [a], 1))

    def act(out, a, f, bias=None, scale=None, extra=0.0):
        def fn(g, T):
            kw = {}
            if bias is not None:
                kw["bias"] = _ap(T, bias)
            if scale is not None:
                kw["scale"] = _ap(T, scale)
            return [g.scalar.activation(_ap(T, out), _ap(T, a), f, **kw)]
        return add("a", fn, [out], [a, bias, scale], 0.065 + extra + max(64, _n(out) * (GATHER if a[0] == "*" else 1)) * CYC)

    ts1, cp1, act1 = ts, cp, act

    def both(i, j):
        o = ops.pop(j)
        ops[i]["alt"] = (o["eng"], o["fn"], o["cost"])
        return i

    def flt(*rs):
        return all(SCRATCH[(r[1] if r[0] == "*" else r)[0]][2] in (F32, F16, B16) for r in rs) and rs[0][0] != "*"

    def act(out, a, f, bias=None, scale=None, extra=0.0):
        i = act1(out, a, f, bias, scale, extra)
        if f == AF.Copy:
            return both(i, cp1(out, a) if scale is None else ts1(out, a, scale, A.mult))
        if f == AF.Identity:
            return both(i, ts1(out, a, bias, A.add))
        if f == AF.Sign:
            return both(i, ts1(out, a, -1.0, A.max, 1.0, A.min))
        return i

    def cp(out, a):
        i = cp1(out, a)
        return both(i, act1(out, a, AF.Copy)) if flt(out, a) else i

    def ts(out, a, s1, o0, s2=None, o1=None):
        i = ts1(out, a, s1, o0, s2, o1)
        if flt(out, a) and o1 is None and o0 == A.mult and not (isinstance(s1, tuple) and _ps(s1)):
            return both(i, act1(out, a, AF.Copy, scale=s1))
        if flt(out, a) and (s1, s2) == (-1.0, 1.0):
            return both(i, act1(out, a, AF.Sign))
        return i

    def lin(out, a, scale, bias):
        i = act1(out, a, AF.Identity, bias=bias, scale=scale)
        return both(i, ts1(out, a, scale, A.mult, bias, A.add))

    def mm(items, first=True, last=True):
        def fn(g, T):
            res = []
            for k, (o, l, r) in enumerate(items):
                st = first if k == 0 else items[k - 1][0] != o
                sp = last if k == len(items) - 1 else items[k + 1][0] != o
                res.append(g.tensor.matmul(_ap(T, o), _ap(T, l), _ap(T, r), st, sp))
            return res
        cost = 0.03 + sum(max(64, _n(r)) * PEC * (4 if SCRATCH[r[0]][2] == F32 else 1) for _, _, r in items)
        return add("t", fn, [o for o, _, _ in items], [l for _, l, _ in items] + [r for _, _, r in items], cost, len(items))

    ndma = [0]

    def dma(fn, wr, rd, cost=2.2):
        ndma[0] += 1
        return add("s", fn, wr, rd, cost, sem="dma%d" % (ndma[0] - 1))

    def exchange(s, parts):
        name, at = ("mw", 0) if s == NP else ("win", s * W)
        k = add("g", ("send", s, parts), [], [R(name, at + CUT[h], at + CUT[h + 1]) for h in parts], SEND, ninc=0)
        for h in parts:
            add("x", None, [R(name, at + V + G * b + CUT[h], at + V + G * b + CUT[h + 1]) for b in range(4)], [],
                XLAT if len(parts) == 2 else XHALF[h], after=[k], sem="arr%d%s" % (s, "ab"[h]))
        return k

    def m16(k):
        return R("m16", 128 * k, 128 * k + 128)

    def mb(k):
        return R("mb", 128 * k, 128 * k + 128)

    def col(k):
        return R("col", k, k + 1)

    SEL, NI16, CF, CW, I16, I16S = 0, 16, 17, 21, 23, 24
    N64, N1024, CMI, LTRI, WAD, BM4, WPA, WPD, BLK, IB, LW = range(11)
    cP, cG, cI, cR, cT, cQ4, cTQ, cFA, cFC, cFB, cFD, cAD = range(12)

    def win(s, lo=0, hi=W):
        return R("win", s * W + lo, s * W + hi)

    def row(i):
        return R("e16", 15 - i, 143 - i)

    def diag(out, name, lo, hi):
        return [(out, row(i), R(name, lo + i, hi, 16)) for i in range(16)]

    def centred(f, out, s, src):
        return f(out, src, AF.Copy) if s else f(out, src, AF.Identity, bias=-2048.0)

    dma(lambda q, T: q.dma_start(T.win[:, 0:G], T.x[:, 0:G]), [win(0, 0, G)], [])
    dma(lambda q, T: q.dma_start(T.nbi[:], T.nb[:]), [R("nbi")], [])
    dma(lambda q, T: q.dma_start(T.win[:, G:V], T.x[:, G:V]), [win(0, G, V)], [], 2.8)
    for k, nm in enumerate(("lb", "pk", "pl", "hq", "pj")):
        dma(lambda q, T, k=k, nm=nm: q.dma_start(T.l32[:, 8 * k:8 * k + 8], T[nm][:]), [R("l32", 8 * k, 8 * k + 8)], [])
    dma(lambda q, T: q.dma_start(T.mw[:, 0:V], T.am[:]), [R("mw", 0, V)], [], 2.6)
    dma(lambda q, T: q.dma_start(T.xi[:], T.x[:]), [R("xi")], [], 4.0)
    add("g", lambda g, T: [g.iota(T.pi[:, 0:1], [[0, 1]], 0, 1)], [R("pi", 0, 1)], [], 0.27)
    add("g", lambda g, T: [g.iota(T.ji[:], [[1, 144]], 0, 0)], [R("ji")], [], 0.45)
    k0 = exchange(0, (0, 1))
    add("g", lambda g, T: [g.iota(T.tab[:], [[1, V]], 0, 0)], [R("tab")], [], 2.7, after=[k0])
    exchange(NP, (0, 1))
    cp(R("off", 0, 320), R("nbi"))
    ts(R("nb16"), R("nbi"), -C0, A.add)

    p0 = R("pi", 0, 1)
    ts(R("pi", 1, 2), p0, 4, A.arith_shift_right)
    ts(R("pi", 2, 3), p0, 15, A.bitwise_and)
    ts(R("pi", 3, 4), p0, 2, A.arith_shift_right, 3, A.bitwise_and)
    ts(R("pi", 4, 5), p0, 3, A.bitwise_and)
    ts(R("pi", 5, 6), p0, 2, A.arith_shift_right)
    cp(R("col", 0, 6), R("pi", 0, 6))
    cp(R("jf"), R("ji"))
    ts(R("i32m"), R("jf", 0, 128), col(cP), A.is_equal)
    ts(R("ti"), R("ji", 0, 128), 4, A.arith_shift_right)
    ts(R("jt", 0, 128), R("ti"), col(cG), A.is_equal)
    blk, eye = R("jt", 0, 128), R("i32m")
    ts(R("mq"), R("jf", 0, 16), col(cI), A.is_equal)
    ts(R("mr"), R("jf", 0, 4), col(cR), A.is_equal)
    cp(m16(I16), eye)
    cp(mb(BLK), blk)
    for q in range(16):
        if q % 2:
            ts(m16(SEL + q), mb(BLK), R("mq", q, q + 1), A.mult)
        else:
            act(m16(SEL + q), blk, AF.Copy, scale=R("mq", q, q + 1))
    ms(R("nbw", 5120, 5376), -C0)
    banks = ["L0", "L1", "L2", "T0", "T1"]
    for q in range(16):
        b = R(banks[q % 5], 0, 320)
        mm([(b, m16(SEL + q), R("nb16"))])
        if q % 2:
            cp(R("nbw", 320 * q, 320 * q + 320), b)
        else:
            act(R("nbw", 320 * q, 320 * q + 320), b, AF.Copy)
    ts(col(16), col(cP), 15.0, A.add)
    ts(R("e16"), R("jf"), col(16), A.is_equal, R("mq", 0, 1), A.mult)
    ts(col(17), col(cG), 16.0, A.mult, 15.0, A.add)
    ts(R("fb16"), R("jf"), col(17), A.is_equal)
    ms(R("ones"), 1.0)
    act(m16(I16S), eye, AF.Copy, scale=0.0625)
    for k, c in ((N64, -64.0), (N1024, -1024.0), (CMI, -15.0 / 32), (IB, 1.0)):
        act(mb(k), eye, AF.Copy, scale=c)
    for lo, hi in CH:
        centred(act, R("x16", lo, hi), 0, win(0, lo, hi))
    act(m16(NI16), eye, AF.Copy, scale=-1.0)
    red(col(cFA), R("mq", 4, 7))
    red(col(12), R("mq", 7, 9))
    red(col(13), R("mq", 9, 12))
    red(col(14), R("mq", 5, 8, 2))
    red(col(15), R("mq", 6, 9, 2))
    ts(col(cFB), col(12), R("mq", 4, 5), A.subtract, R("mr", 3, 4), A.subtract)
    ts(col(cFC), col(13), col(14), A.subtract, R("mr", 0, 1), A.subtract)
    ts(col(cFD), col(15), col(13), A.add, -1.0, A.mult)
    ts(col(cAD), R("mr", 0, 1), R("mr", 3, 4), A.add)
    for r, c in enumerate((cFA, cFC, cFB, cFD)):
        act(m16(CF + r), eye, AF.Copy, scale=col(c))
    ts(m16(CW), m16(I16), R("mr", 0, 1), A.mult, -1.0, A.mult)
    ts(m16(CW + 1), m16(I16), R("mr", 3, 4), A.mult, -1.0, A.mult)
    ts(R("ti"), R("ji", 0, 128), 2, A.arith_shift_right)
    ts(R("tb"), R("ti"), col(cQ4), A.is_equal)
    ts(R("tw"), R("jf", 0, 128), col(cP), A.is_gt)
    tt(mb(LTRI), R("tb"), R("tw"), A.mult)
    act(mb(WAD), blk, AF.Copy, scale=col(cAD))
    act(mb(BM4), blk, AF.Copy, scale=-4.0)
    ts(col(cTQ), col(cT), 80.0, A.mult, 1.0, A.add)
    ts(mb(WPA), mb(BLK), col(cTQ), A.mult, R("mr", 0, 1), A.mult)
    ts(mb(WPD), mb(BLK), col(cTQ), A.mult, R("mr", 3, 4), A.mult)
    ts(R("spare"), R("jf", 0, 16), 16.0, A.mult, col(cI), A.add)
    ln2 = math.log(2.0)
    ts(R("vt", 0, 4), R("spare", 0, 4), -2 * ln2, A.mult, 64 * ln2, A.add)
    act(R("w4"), R("vt", 0, 4), AF.Exp, extra=1.3)
    ts(R("thg"), R("jf", 0, 64), -2 * ln2, A.mult, 64 * ln2 + math.log(6.5), A.add)
    act(R("thr"), R("thg"), AF.Exp)
    ts(R("spare"), R("spare"), 5120.0, A.add)
    cp(R("lu"), R("l32"))
    cp(R("lf"), R("l32"))
    cp(R("rep", 0, 128), IND(R("tab"), R("lu", 0, 8)))
    ts(R("lq16"), R("lf", 16, 24), 0.25, A.mult)
    ts(R("ti", 0, 8), R("l32", 0, 8), 4, A.arith_shift_right)
    ts(R("tw", 0, 8), R("ti", 0, 8), -5119.0, A.mult)
    ts(R("tb", 0, 8), R("lf", 0, 8), 320.0, A.mult)
    tt(R("to", 0, 8), R("tb", 0, 8), R("tw", 0, 8), A.add)
    ts(R("tw", 0, 8), R("lf", 8, 16), 80.0, A.mult)
    ts(R("tw", 8, 16), R("lf", 32, 40), 80.0, A.mult)
    for t in range(2):
        for h in range(2):
            tt(R("o1f", 8 * t + 4 * h, 8 * t + 4 * h + 4), R("to", 4 * t, 4 * t + 4), R("tw", 8 * h + 4 * t, 8 * h + 4 * t + 4), A.add)
        ts(R("at16", 256 * t + 128, 256 * t + 192), R("rep", 64 * t, 64 * t + 64), -C0, A.add)
    cp(R("o1"), R("o1f"))
    ts(R("vt"), R("lf", 8, 24), -80.0, A.mult)
    for t in range(2):
        cp(R("pt", 16 * t, 16 * t + 4), R("spare", 0, 4))
        cp(R("pt", 16 * t + 12, 16 * t + 16), R("spare", 0, 4))
        tt(R("pt", 16 * t + 4, 16 * t + 8), R("vt", 8 + 4 * t, 12 + 4 * t), R("spare", 0, 4), A.add)
        tt(R("pt", 16 * t + 8, 16 * t + 12), R("vt", 4 * t, 4 * t + 4), R("spare", 0, 4), A.add)

    HI0, B0 = C0 / 16 - 0.4921875, 320.0 * C0

    def place(v, n, at):
        ts(R("ti", at, at + n), v, 0.0625, A.mult, HI0, A.add)
        ts(R("tb", at, at + n), v, 320.0, A.mult, B0, A.add) if n == 4 else lin(R("tb", at, at + n), v, 320.0, B0)

    def place_sum(out, n, at):
        ts(R("tw", at, at + n), R("ti", at, at + n), -5119.0, A.mult)
        tt(out, R("tw", at, at + n), R("tb", at, at + n), A.add)

    nbw = R("nbw")

    def names(h):
        act1(R("nm16", 0, 512), IND(nbw, R("o2", 0, 32)), AF.Copy)
        if h or NM0 == "a":
            act(R("nm16", 512, 1024), IND(nbw, R("o2", 32, 64)), AF.Copy)
        else:
            cp1(R("nm16", 512, 1024), IND(nbw, R("o2", 32, 64)))

    def names_list(h):
        mm(diag(R("L1", 256, 320), "nm16", 0, 1024))
        lin(R("o4", 64 * h, 64 * h + 64), R("L1", 256, 320), 1.0, C0)

    def switch(flag, h, t, dst):
        for c in range(4):
            ts(R("osc", 16 * h + c, 16 * h + 16, 4), R("dn", c, 16, 4), R(flag[0], flag[1] + c, flag[1] + c + 1), A.mult, R("spare", c, c + 1), A.add)
        for k, u in enumerate((2, 3, 0, 1) if h else (1, 0, 3, 2)):
            cp(IND(nbw, R("osc", 16 * h + 4 * u, 16 * h + 4 * u + 4)), R("at16", 256 * t + 64 * k, 256 * t + 64 * k + 64))
        dma(lambda q, T: q.dma_start(T.off32[:], T.nbw[0:128:18, 0:5120]), [R("off32")], [R("nbw", 0, 5120)], 2.8)
        lin(R("off", 320 * dst, 320 * dst + 320), R("off32"), 1.0, C0)

    def lanes(t, dst):
        a0 = 256 * t

        def at(r):
            return R("at16", a0 + 64 * r, a0 + 64 * r + 64)
        cp(R("at16", a0, a0 + 128), IND(nbw, R("o1", 8 * t, 8 * t + 8)))
        pl = R("L2", 0, 4)
        mm(diag(pl, "at16", a0 + 64, a0 + 128) + [(pl, m16(I16), R("lq16", 4 * t, 4 * t + 4))])
        place(pl, 4, 64)
        for c in range(4):
            ts(R("oc", c, c + 1), R("ti", 64 + c, 65 + c), -5119.0, A.mult, R("tb", 64 + c, 65 + c), A.add)
        cp(at(3), IND(nbw, R("oc")))
        pc = R("L2", 64, 80)
        mm(diag(pc, "at16", a0, a0 + 256))
        place(pc, 16, 0)
        cp(R("al"), pc)
        place_sum(R("to", 0, 16), 16, 0)
        for p in range(4):
            ts(R("o2", 16 * p, 16 * p + 16), R("to", 0, 16), 80.0 * p, A.add)
        ts(R("eg"), R("at16", a0, a0 + 256), -128.0, A.is_ge)
        ts(R("o3"), R("al"), C0, A.add, V - 1.0, A.min)
        names(0)
        tt(R("dn"), R("to", 0, 16), R("pt", 16 * t, 16 * t + 16), A.subtract)
        uf, uw, n2 = R("L0", 0, 64), R("L0", 64, 128), R("L2", 128, 192)
        ad = [(i, R("nm16", 64 * (4 * (i % 4) + i // 4), 64 * (4 * (i % 4) + i // 4 + 1))) for i in (0, 1, 2, 3, 12, 13, 14, 15)]
        mm([(uf, m16(CF + r), at(r)) for r in range(4)] + [(uw, m16(CW), at(2)), (uw, m16(CW + 1), at(1))])
        act(R("tm"), R("L0", 0, 128), AF.Copy, scale=-1.0)
        mm([(n2, row(i), u) for i, u in ad])
        tt(R("eb", 64, 128), n2, R("tm", 64, 128), A.is_equal)
        tt(R("eb", 0, 64), n2, R("tm", 0, 64), A.is_equal)
        mm([(R("L2", 256, 320), mb(LTRI), R("eb", 64, 128))])
        chg = R("eb", 128, 192)
        tt(chg, R("eb", 64, 128), R("L2", 256, 320), A.is_gt)
        sc = R("L2", 0, 64)
        mm([(sc, mb(N64), R("eg", 64 * r, 64 * r + 64)) for r in (0, 1, 3)] + [(sc, mb(BM4), R("eb", 0, 64)), (sc, mb(WAD), chg),
            (R("L2", 64, 128), mb(WPA), chg), (R("L2", 128, 192), mb(WPD), chg)])
        both(act1(R("gp16"), R("L2", 0, 192), AF.Relu, bias=-1.0), ts1(R("gp16"), R("L2", 0, 192), -1.0, A.add, 0.0, A.max))
        for r in range(4):
            for c in range(4):
                k = 4 * c + r
                ts(R("eq", 256 * k, 256 * k + 256), R("at16", a0, a0 + 256), R("al", 4 * r + c, 4 * r + c + 1), A.is_equal)
        for c in range(4):
            mm([(R("L1", 64 * c, 64 * c + 64), mb(IB), R("eq", 1024 * c + 64 * k, 1024 * c + 64 * k + 64)) for k in range(16)])
        act(R("sb"), R("L1", 0, 256), AF.Copy)
        names_list(0)
        mm(diag(R("L2", 320, 332), "gp16", 0, 192))
        for c in range(4):
            ts(mb(LW + c), mb(BLK), R("L2", 320 + c, 321 + c), A.mult, R("w4", c, c + 1), A.mult)
        tt(R("dn", 0, 4), R("L2", 324, 328), R("dn", 0, 4), A.add)
        tt(R("dn", 12, 16), R("L2", 328, 332), R("dn", 12, 16), A.add)
        mm([(R("L2", 384, 448), mb(LW + c), R("sb", 64 * c, 64 * c + 64)) for c in range(4)])
        tt(R("thg"), R("thr"), R("gp16", 0, 64), A.mult)
        tt(R("wn16", 0, 64), R("L2", 384, 448), R("thg"), A.is_lt)
        mm(diag(R("L2", 480, 484), "wn16", 0, 64))
        switch(R("L2", 480, 484), 0, t, dst)
        lin(R("hqw", 0, 4), R("L2", 480, 484), -99.0, 99.0)
        tt(R("hqw", 4, 8), R("hqw", 0, 4), R("lf", 24 + 4 * t, 28 + 4 * t), A.add)

    def stress(s, h):
        centred(act, R("xo"), s, IND(win(s, 0, V), R("o3")))
        for u in range(2):
            a, b = 512 * u, 512 * u + 512
            bk = "L%d" % u
            if STRESS[s // 3 * 2 + h][u] == "a":
                centred(act, R("ld", a, b), s, IND(win(s), R("o4", 64 * h + 32 * u, 64 * h + 32 * u + 32)))
                for v in range(2):
                    o = R(bk, 256 * v, 256 * v + 256)
                    mm([(o, m16(I16), R("ld", a + 256 * v, a + 256 * v + 256)), (o, m16(NI16), R("xo"))])
                ts(R("lc", a, b), R(bk), -2047.0, A.max, 2047.0, A.min)
            else:
                for v in range(2):
                    at = 64 * h + 32 * u + 16 * v
                    tt(R("ld", a + 256 * v, a + 256 * v + 256), IND(win(s), R("o4", at, at + 16)), R("xo"), A.subtract)
                ts(R("lc", a, b), R("ld", a, b), -2047.0, A.max, 2047.0, A.min)
            ts(R("ls", a, b), R("lc", a, b), -1.0, A.max, 1.0, A.min)
            mm([(R(bk), m16(I16), R("lc", a, b)), (R(bk), mb(N1024), R("ls", a, b))])
            act(R("sq", a, b), R(bk), AF.Square)
        for u in range(2):
            mm([(R("L0", 0, 64), R("i32m"), R("sq", 512 * u + 64 * v, 512 * u + 64 * v + 64)) for v in range(8)], first=u == 0, last=u == 1)
        if h == 0:
            act(R("sf"), R("L0", 0, 64), AF.Copy)

    def votes(t, dst):
        tt(R("wb"), R("L0", 0, 64), R("sf"), A.is_gt)
        mm([(R("L2", 384, 388), R("fb16", 15 - i, 143 - i), R("wb", i, 64, 16)) for i in range(16)])
        tt(R("hqw", 8, 12), R("L2", 384, 388), R("hqw", 4, 8), A.is_ge)
        switch(R("hqw", 8, 12), 1, t, dst)

    turn = [0, 0]

    def diffs(s, k, o):
        lo, hi, nact, onv = k
        m = hi - lo
        b = turn[0] % NSET
        turn[0] += 1

        def sl(name, p, n=1):
            return R(name, 4 * CM * b + m * p, 4 * CM * b + m * (p + n))

        def offs(p):
            return IND(win(s), R("off", 320 * o + 80 * p + lo // 16, 320 * o + 80 * p + hi // 16))
        for p in range(4 - nact, 4):
            xk = R("X%d" % (turn[1] % 3), 0, m)
            turn[1] += 1
            centred(act1, sl("d16", p), s, offs(p))
            mm([(xk, m16(NI16), R("x16", V * s + lo, V * s + hi)), (xk, m16(I16), sl("d16", p))])
            ts(sl("c16", p), xk, -2047.0, A.max, 2047.0, A.min)
        for p in range(4 - nact):
            tt(sl("d16", p), offs(p), R("x16", V * s + lo, V * s + hi) if s else R("xi", lo, hi), A.subtract)
        one = s == NP - 1
        mine = [(p, 1) for p in range(4 - nact)] if one or nact == 4 else [(0, 4 - nact)]
        for p, n in mine:
            ts(sl("c16", p, n), sl("d16", p, n), -2047.0, A.max, 2047.0, A.min)
        for p, n in mine + ([(p, 1) for p in range(4 - nact, 4)] if one or lo < G else [(4 - nact, nact)]):
            src = sl("d16" if p + n <= 4 - nact else "c16", p, n)
            if p in onv:
                ts(sl("s16", p, n), src, -1.0, A.max, 1.0, A.min)
            else:
                act(sl("s16", p, n), src, AF.Sign)
        return sl

    def sweep(s, o):
        xa, xb = V * s, V * (s + 1)
        for k in (SUB0, SUB1, SUB2)[s % 3]:
            lo, hi = k[:2]
            m = hi - lo
            tb = R("T%d" % (turn[0] % 2), 0, m)
            mm([(tb, m16(I16), R("x16", xa + lo, xa + hi)), (tb, mb(CMI), R("ones", 0, m))], last=False)
            sl = diffs(s, k, o)
            for kind, p in ("c0", "c1", "s0", "s1", "c2", "s2", "c3", "s3") if lo < G else ("c0", "c1", "s0", "s1", "c2", "c3", "s2", "s3"):
                mm([(tb, m16(I16S) if kind == "c" else mb(N64), sl(kind + "16", int(p)))], first=False, last=kind + p == "s3")
            ts(win(s + 1, lo, hi), tb, -2048.0, A.max, 2047.0, A.min)
            sent = [exchange(s + 1, (CUT.index(lo),))] if hi <= G else []
            if hi < G:
                continue
            if hi == G:
                lo, m = 0, G
            add("g", lambda g, T, lo=lo, hi=hi: [g.affine_select(T.x16[:, xb + lo:xb + hi], _ap(T, win(s + 1, lo, hi)), [[0, hi - lo]], A.is_equal, 0.0, 0, 0)],
                [R("x16", xb + lo, xb + hi)], [win(s + 1, lo, hi)], 0.2 + 2 * m * CYC, after=sent)

    def final(s, o):
        nf = 0
        for k in FSUB:
            lo, hi = k[:2]
            m = hi - lo
            yb = R("T%d" % (turn[0] % 2), 0, m)
            sl = diffs(s, k, o)
            for p in (3, 0, 1, 2):
                fb = R("L%d" % (nf % 3), 0, m)
                e = R("fe", CM * (nf % 4), CM * (nf % 4) + m)
                tq = R("fq", CM * (nf % 4), CM * (nf % 4) + m)
                nf += 1
                mm([(fb, m16(I16), sl("c16", p)), (fb, mb(N1024), sl("s16", p))])
                act(e, fb, AF.Square)
                act(e, e, AF.Exp, scale=-2.0 ** -19)
                tt(tq, IND(R("mw"), R("off", 320 * o + 80 * p + lo // 16, 320 * o + 80 * p + hi // 16)), e, A.mult)
                if p != 2:
                    mm([(yb, R("i32m"), tq)], first=p == 3, last=p == 1)
            tt(R("fy", lo, hi), yb, tq, A.add)
            dma(lambda q, T, lo=lo, hi=hi: q.dma_start(T.y[:, lo:hi], T.fy[:, lo:hi]), [], [R("fy", lo, hi)])

    for t in range(2):
        lanes(t, 2 * t + 1)
        stress(3 * t, 0)
        names(1)
        names_list(1)
        sweep(3 * t, 2 * t)
        sweep(3 * t + 1, 2 * t + 1)
        stress(3 * t + 2, 1)
        votes(t, 2 * t + 2)
        sweep(3 * t + 2, 2 * t + 1)
    final(6, 4)
    return ops


def schedule(ops):
    hist = {}
    for i, o in enumerate(ops):
        deps = set(o["after"])
        acc = [(r, True) for r in o["w"]] + [(r, False) for r in o["r"]]
        for r, wr in acc:
            ps = _ps(r)
            for j, lo, hi, w2, st in hist.get(r[0], []):
                if ps:
                    if wr or w2 or ops[j]["eng"] != o["eng"] or "alt" in o or "alt" in ops[j]:
                        deps.add(j)
                elif (wr or w2) and lo < r[2] and r[1] < hi and not (st == r[3] > 1 and (lo - r[1]) % st):
                    deps.add(j)
        for r, wr in acc:
            h = hist.setdefault(r[0], [])
            if wr and (r[3] == 1 or _ps(r)):
                h[:] = [] if _ps(r) else [e for e in h if not (r[1] <= e[1] and e[2] <= r[2])]
        for r, wr in acc:
            hist[r[0]].append((i, r[1], r[2], wr, r[3]))
        deps.discard(i)
        o["deps"] = sorted(deps)
    n = len(ops)

    pred = [o["deps"] for o in ops]
    succ = [[] for _ in range(n)]
    for i in range(n):
        for j in pred[i]:
            succ[j].append(i)
    forms = [[(o["eng"], o["cost"])] + ([(o["alt"][0], o["alt"][2])] if "alt" in o else []) for o in ops]
    two = [i for i in range(n) if len(forms[i]) > 1]

    def lat(a, b):
        return 0.0 if a == b == "t" or b == "x" else (SAME if a == b else CROSS)

    def pack(keys, before, form, back):
        starts, ends = {e: [] for e in "vatg"}, {e: [] for e in "vatg"}
        fin = [None] * n
        for i0 in sorted(range(n), key=lambda i: -keys[i]):
            todo = [i0]
            while todo:
                i = todo[-1]
                if fin[i] is not None:
                    todo.pop()
                    continue
                late = [j for j in before[i] if fin[j] is None]
                if late:
                    todo += late
                    continue
                e, c = forms[i][form[i]]
                st = 0.0
                for j in before[i]:
                    ej = forms[j][form[j]][0]
                    u = fin[j] + (lat(e, ej) if back else lat(ej, e))
                    if u > st:
                        st = u
                if e in starts:
                    ss, es = starts[e], ends[e]
                    at, top = 0, len(es)
                    while at < top:
                        mid = (at + top) // 2
                        if es[mid] > st:
                            top = mid
                        else:
                            at = mid + 1
                    while at < len(ss) and st + c > ss[at] + 1e-9:
                        if es[at] > st:
                            st = es[at]
                        at += 1
                    ss.insert(at, st)
                    es.insert(at, st + c)
                fin[i] = st + c
        return fin
    keys = [0.0] * n
    for i in range(n - 1, -1, -1):
        keys[i] = forms[i][0][1] + max([keys[k] + lat(forms[i][0][0], forms[k][0][0]) for k in succ[i]] + [0.0])
    state = [SEED]

    def draw():
        state[0] = (state[0] * 1103515245 + 12345) % 2147483648
        return state[0] / 2147483648.0
    best, now, kept = None, None, [0] * n
    for it in range(ROUNDS):
        form = list(kept)
        for _ in range(1 + int(draw() * FLIPS) if it else 0):
            i = two[int(draw() * len(two))]
            form[i] = 1 - form[i]
        a = draw() * NOISE
        fin = pack(pack([k + a * draw() for k in keys], pred, form, False), succ, form, True)
        end = pack(fin, pred, form, False)
        if now is None or max(end) < now + TEMP * (1 - it / ROUNDS) * draw():
            now, kept, keys = max(end), form, fin
        if best is None or max(end) < best[0]:
            best = (max(end), end, form)
    _, end, form = best
    for i, o in enumerate(ops):
        if form[i]:
            o["eng"], o["fn"], o["cost"] = o["alt"]
        o["start"] = end[i] - o["cost"]
    seq = sorted(range(n), key=lambda i: (round(ops[i]["start"], 6), i))
    order = {e: [i for i in seq if ops[i]["eng"] == e] for e in "vatgsx"}
    count = {e: 0 for e in "vatg"}
    known = {e: {} for e in "vatgs"}
    clock = [None] * n
    for i in seq:
        o = ops[i]
        e = o["eng"]
        if e == "x":
            o["tag"] = (o["sem"], 16)
            clock[i] = {o["sem"]: 16}
            continue
        kn = known[e]
        waits = []
        for j in sorted(o["deps"], key=lambda j: -end[j]):
            d = ops[j]
            if d["tag"] is None or (e == "t" and d["eng"] == "t"):
                continue
            s, c = d["tag"]
            if kn.get(s, 0) < c:
                waits.append((s, c))
                for s2, c2 in clock[j].items():
                    kn[s2] = max(kn.get(s2, 0), c2)
        o["waits"] = waits
        if e == "s":
            o["tag"] = (o["sem"], 16)
        elif o["ninc"]:
            count[e] += o["ninc"]
            o["tag"] = ("q" + e, count[e])
        else:
            o["tag"] = None
        clock[i] = dict(kn)
        if o["tag"]:
            clock[i][o["tag"][0]] = o["tag"][1]
    return order, count, max(end)


OPS = build()
ORDER, COUNT, SPAN = schedule(OPS)


def _mask(engs):
    return sum(1 << e for e in engs)


def helpers(core, T, topo):
    r = T.rank_of(core)
    dsts = [T.cores[(r + d) % len(T.cores)] for d in DS]
    hs = [c for c in topo.cores_of(core) if c != core and all(topo.may_write(c, d) for d in dsts)]
    hs.sort(key=lambda c: (topo.die(c) == topo.die(core), c))
    return hs[:4], dsts


def _slot(T, s, row):
    return T.hopm[row:row + 128, :] if s == NP else T.hop[256 * s + row:256 * s + row + 128, :]


def _cols(T, s, lo):
    return T.mw[:, lo:lo + H] if s == NP else T.win[:, s * W + lo:s * W + lo + H]


def helper_program(g, core, owner, T, topo):
    hs, dsts = helpers(owner, T, topo)
    k = hs.index(core)
    total = 0
    for s in [0, NP] + list(range(1, NP)):
        g.wait_ge(T.sem["rel%d" % s], 8 if s in (0, NP) else 16)
        trs = []
        for u in range(2):
            b = 2 * (k % 2) + u
            rid, pid = topo.addr(dsts[b], core)
            engs = topo.engines(core, dsts[b])
            trs.append(RemoteDMATransfer(dst_ids=[DstId(rid=rid, pnc=pid)], dma_engine_mask=_mask(engs[4 * u:4 * u + 4]),
                                         remote_sem=T.sem["arr%d%s" % (s, "ab"[k // 2])], src=_slot(T, s, 16 * b),
                                         dst=_cols(T, s, V + G * b + H * (k // 2))))
        g.remote_dma_fused(trs, local_sem=T.sem.sent)
        total += 8
    g.wait_ge(T.sem.sent, total)


def rank_program(g, core, T, topo):
    if T.rank_of(core) is None:
        for owner in topo.cores_of(core):
            if T.rank_of(owner) is not None and core in helpers(owner, T, topo)[0]:
                helper_program(g, core, owner, T, topo)
        return
    hs, _ = helpers(core, T, topo)
    queue = {"v": g.vector, "a": g.scalar, "t": g.tensor, "g": g, "s": g.sync}
    sent = 0
    for e in "svatg":
        q = queue[e]
        for i in ORDER[e]:
            o = OPS[i]
            for s, c in o["waits"]:
                q.wait_ge(T.sem[s], c)
            if e == "s":
                o["fn"](q, T).then_inc(T.sem[o["sem"]], 16)
            elif isinstance(o["fn"], tuple):
                _, s, parts = o["fn"]
                trs = []
                for k, h in enumerate(hs):
                    if k // 2 not in parts:
                        continue
                    rid, pid = topo.addr(h, core)
                    engs = topo.engines(core, h)
                    if len(parts) == 2:
                        engs = engs[k // 2::2]
                    n = len(engs) // 2
                    trs.append(RemoteDMATransfer(dst_ids=[DstId(rid=rid, pnc=pid)] * 2, dma_engine_mask=_mask(engs[n * (k % 2):n * (k % 2) + n]),
                                                 remote_sem=T.sem["rel%d" % s], srcs=[_cols(T, s, H * (k // 2))],
                                                 dsts=[_slot(T, s, 0), _slot(T, s, 128)]))
                g.remote_dma_fused(trs, local_sem=T.sem.sent)
                sent += 16
            else:
                for ins in o["fn"](g, T):
                    ins.then_inc(T.sem["q" + e], 1)
    for e in "vatg":
        g.wait_ge(T.sem["q" + e], COUNT[e])
    for i in ORDER["s"] + ORDER["x"]:
        g.wait_ge(T.sem[OPS[i]["tag"][0]], OPS[i]["tag"][1])
    g.wait_ge(T.sem.sent, sent)
